import numpy as np
import ml_dtypes


def mxq(x, axis, fmt="e4m3"):
    dtype, down = {"e4m3": (ml_dtypes.float8_e4m3fn, 7), "e5m2": (ml_dtypes.float8_e5m2, 14)}[fmt]
    v = np.moveaxis(np.asarray(x, np.float32).astype(ml_dtypes.bfloat16).astype(np.float64), axis, -1)
    blocks = v.reshape(v.shape[:-1] + (-1, 32))
    amax = np.abs(blocks).max(-1, keepdims=True)
    byte = np.maximum(np.where(amax > 0, np.frexp(amax)[1] - 1 + 127, 0) - down, 1)
    scale = np.exp2(byte - 127.0)
    codes = (blocks / scale).astype(np.float32).astype(dtype).astype(np.float64)
    return np.moveaxis((codes * scale).reshape(v.shape), -1, axis)


WIDE = False


def mx_kscale(k):
    if not WIDE:
        return np.ones(k)
    levels = np.array([10, -10, 5, -5, 0])
    if k % 512:
        return np.exp2(np.random.permutation(np.resize(levels, k // 32))).repeat(32)
    a = np.empty((k // 512, 16))
    for p in range(k // 512):
        a[p, :8] = np.random.permutation(np.resize(levels, 8))
        for g in range(8):
            far = levels[np.abs(levels - a[p, g]) >= 10]
            a[p, g + 8] = far[np.random.randint(len(far))]
    return np.exp2(a.ravel()).repeat(32)


def f64(x):
    return np.asarray(x).astype(np.float64)


def striped(idx):
    return np.tile(idx.reshape(-1, 16).T, (8, 1)).astype(np.uint16)


def unstriped(offs):
    return offs[:16].T.reshape(-1).astype(np.int64)


E2M1 = np.array([0.0, 0.5, 1.0, 1.5, 2.0, 3.0, 4.0, 6.0, -0.0, -0.5, -1.0, -1.5, -2.0, -3.0, -4.0, -6.0])


def pack_weight(w, fmt):
    k, n = w.shape
    w = f64(np.asarray(w, np.float32).astype(ml_dtypes.bfloat16)).reshape(k // 32, 32, n)
    amax = np.abs(w).max(1)
    if fmt == "e4m3":
        byte = np.frexp(amax)[1] - 1 + 127 - 7
    else:
        mant, ex = np.frexp(amax / 6.0)
        byte = np.where(mant > 0.5, ex, ex - 1) + 127
    byte = np.clip(np.where(amax > 0, byte, 1), 1, 254)
    scaled = (w * np.exp2(127.0 - byte)[:, None, :]).reshape(k, n).astype(np.float32)
    by_word = np.ascontiguousarray(scaled.reshape(k // 512, 128, 4, n).transpose(0, 1, 3, 2))
    if fmt == "e4m3":
        words = by_word.astype(ml_dtypes.float8_e4m3fn).view(np.uint8)
    else:
        c = by_word.astype(ml_dtypes.float4_e2m1fn).view(np.uint8) & 0xF
        words = (c[..., 0::2] | (c[..., 1::2] << 4)).reshape(k // 512, 128, 2 * n)
    return np.ascontiguousarray(words), np.ascontiguousarray(byte.astype(np.uint8).reshape(k // 512, 16, n))


def unpack_weight(words, scales, fmt):
    g, _, n = scales.shape
    words = np.ascontiguousarray(words).reshape(g, 128, n, -1)
    if fmt == "e4m3":
        vals = words.view(ml_dtypes.float8_e4m3fn).astype(np.float64)
    else:
        nib = np.empty((g, 128, n, 4), np.uint8)
        nib[..., 0::2] = words & 0xF
        nib[..., 1::2] = words >> 4
        vals = E2M1[nib]
    vals = vals * np.repeat(np.exp2(scales.astype(np.float64) - 127.0), 8, axis=1)[..., None]
    return vals.transpose(0, 1, 3, 2).reshape(g * 512, n)


def gelu(v):
    return 0.5 * v * (1.0 + np.tanh(np.sqrt(2.0 / np.pi) * (v + 0.044715 * v**3)))


def bf(x):
    return np.asarray(x, np.float32).astype(ml_dtypes.bfloat16)

def planes(Y):
    n, m = Y.shape
    b = f64(bf(Y)).reshape(n // 32, 32, m)
    amax = np.abs(b).max(1)
    byte = np.clip(np.where(amax > 0, np.frexp(amax)[1] - 1 + 127 - 7, 1), 1, 254)
    codes = (b * np.exp2(127.0 - byte)[:, None, :]).reshape(n, m).astype(np.float32).astype(ml_dtypes.float8_e4m3fn).view(np.uint8)
    words = codes.reshape(n // 512, 128, 4, m).transpose(0, 1, 3, 2)
    return np.ascontiguousarray(words), np.ascontiguousarray(byte.astype(np.uint8).reshape(n // 512, 16, m))


K, T, S, H, N = 512, 4096, 1024, 1024, 512

def setup_inputs():
    n = np.random.standard_normal
    s = mx_kscale(K)[:, None]
    u = mx_kscale(H)[:, None]
    tab = np.abs(n((K, T))) * np.exp(0.3 * n(T)) * s
    tab_words, tab_scales = pack_weight(tab, "e4m3")
    w1 = 0.5 * n((K, H)) / np.sqrt(K) / s
    w2 = 0.8 * n((K, H)) ** 2 / K * np.exp(0.4 * n(H)) / s
    w2_words, w2_scales = pack_weight(w2, "e2m1")
    g = np.exp(0.3 * n(H)) * u[:, 0]
    w3 = n((H, N)) / np.sqrt(H) * np.exp(0.8 * n(N)) / u
    return {"tab_words": tab_words, "tab_scales": tab_scales,
            "offs": striped(np.random.permutation(T)[:S]),
            "w1": w1.astype(np.float32),
            "w2_words": w2_words, "w2_scales": w2_scales,
            "g": g.astype(np.float32), "w3": w3.astype(np.float32)}

def reference(tab_words, tab_scales, offs, w1, w2_words, w2_scales, g, w3):
    v = unpack_weight(tab_words, tab_scales, "e4m3")[:, unstriped(offs)]
    w2 = unpack_weight(w2_words, w2_scales, "e2m1")
    a = mxq(f64(w1), 0, "e4m3").T @ v
    b = w2.T @ v
    h = f64(g)[:, None] * np.exp(-(np.exp(a) * b))
    y = mxq(f64(w3), 0, "e4m3").T @ mxq(h, 0, "e4m3")
    words, scales = planes(y)
    return y, words, scales

@@ -1,0 +1,248 @@
+from contextlib import ExitStack
+
+import concourse.mybir as mybir
+
+K, T, S, H, N = 512, 4096, 1024, 1024, 512
+FLOPS = 2 * (2 * K * H * S + H * N * S)
+
+F32 = mybir.dt.float32
+BF16 = mybir.dt.bfloat16
+I32 = mybir.dt.int32
+U32 = mybir.dt.uint32
+U16 = mybir.dt.uint16
+U8 = mybir.dt.uint8
+FP8X4 = mybir.dt.float8_e4m3fn_x4
+FP4X4 = mybir.dt.float4_e2m1fn_x4
+ALU = mybir.AluOpType
+EXP = mybir.ActivationFunctionType.Exp
+
+P = 128
+PACK = 4
+PASS = P * PACK
+UNIT = 128
+HALF = 512
+CHUNKS = [(0, 256), (256, 256), (512, 256), (768, 128), (896, 128)]
+BIG = 3.0e38
+ROW0 = P - 16
+
+
+def tile_list_survival_treatment_scores_kernel(
+    tc, tab_words, tab_scales, offs, w1, w2_words, w2_scales, g, w3, out_0, out_1, out_2
+):
+    nc = tc.nc
+    with ExitStack() as ctx:
+        lists = ctx.enter_context(tc.tile_pool(name="lists", bufs=1))
+        keep = ctx.enter_context(tc.tile_pool(name="keep", bufs=1))
+        raws = ctx.enter_context(tc.tile_pool(name="raws", bufs=1))
+        work = ctx.enter_context(tc.tile_pool(name="work", bufs=3))
+        ps_a = ctx.enter_context(tc.psum_pool(name="ps_a", bufs=3))
+        ps_b = ctx.enter_context(tc.psum_pool(name="ps_b", bufs=3))
+        ps_y = ctx.enter_context(tc.psum_pool(name="ps_y", bufs=2))
+
+        offsets = lists.tile([P, S // 16], U16, name="offsets")
+        nc.sync.dma_start(offsets[:], offs)
+
+        tabs = keep.tile([P, T], U8, name="tabs", align_bytes=64)
+        nc.sync.dma_start(tabs[ROW0:, :].bitcast(I32), tab_scales[0].bitcast(I32))
+        nc.gpsimd.memset(tabs[:ROW0, :].bitcast(I32), 0)
+        w2s_raw = keep.tile([P, H], U8, name="w2s_raw", align_bytes=64)
+        nc.sync.dma_start(w2s_raw[ROW0:, :].bitcast(I32), w2_scales[0].bitcast(I32))
+        nc.gpsimd.memset(w2s_raw[:ROW0, :].bitcast(I32), 0)
+        planes = keep.tile([P, S + H], U8, name="planes", align_bytes=64)
+        nc.gpsimd.memset(planes[:].bitcast(I32), 0)
+        gt = keep.tile([P, 2, PACK], F32, name="gt")
+        nc.scalar.dma_start(gt[:], g.rearrange("(b p t) -> p b t", t=PACK, p=P))
+
+        w2_raw = keep.tile([P, 2 * H], U8, name="w2_raw", align_bytes=64)
+        nc.sync.dma_start(w2_raw[:].bitcast(I32), w2_words[0].bitcast(I32))
+        tabw = keep.tile([P, T], I32, name="tabw", align_bytes=64)
+        nc.sync.dma_start(tabw[:], tab_words[0].rearrange("p t i -> p (t i)").bitcast(I32))
+
+        def load_rows(rows, tag):
+            raw = raws.tile([P, PACK, rows.shape[1]], F32, name="raw", tag=tag, align_bytes=64)
+            nc.sync.dma_start(raw[:], rows.rearrange("(p j) c -> p j c", j=PACK))
+            return raw
+
+        def quantise_weight(name, pieces, calls):
+            grouped = keep.tile([P, PACK * PASS], BF16, name=name + "_bf", align_bytes=64)
+            dst = grouped[:].rearrange("p (t m j) -> p m j t", t=PACK, j=PACK)
+            for engine, raw, first, lo, hi in pieces:
+                src = raw[:].rearrange("p j (m t) -> p m j t", t=PACK)
+                if engine == "vector":
+                    nc.vector.tensor_copy(dst[:, lo:hi], src[:, lo - first : hi - first])
+                else:
+                    nc.scalar.copy(dst[:, lo:hi], src[:, lo - first : hi - first])
+            codes = keep.tile([P, PASS], U32, name=name + "_q", align_bytes=64)
+            scales = keep.tile([P, PASS], U8, name=name + "_s", align_bytes=64)
+            step = PASS // calls
+            for c0 in range(0, PASS, step):
+                nc.vector.quantize_mx(
+                    out=codes[:, c0 : c0 + step].bitcast(FP8X4), scales=scales[:, c0 : c0 + step],
+                    in_=grouped[:, PACK * c0 : PACK * (c0 + step)],
+                )
+            return codes, scales
+
+        w1_lo = load_rows(w1[:, 0 : PASS // 2], "lo")
+        w1_hi = load_rows(w1[:, PASS // 2 : PASS], "early")
+        warm = keep.tile([P, 2], F32, name="warm")
+        nc.vector.memset(warm[:, 0:1], 0.0)
+        nc.scalar.activation(warm[:, 1:2], warm[:, 0:1], EXP)
+
+        w2q = keep.tile([P, 2 * H], U8, name="w2q", align_bytes=64)
+        nc.vector.tensor_copy(
+            w2q[:].bitcast(U16).rearrange("p (b t m) -> p b m t", b=2, t=PACK),
+            w2_raw[:].bitcast(U16).rearrange("p (b m t) -> p b m t", b=2, t=PACK),
+        )
+
+        vq = []
+        picked = keep.tile([P, S], U8, name="picked", align_bytes=64)
+        nc.vector.tensor_copy(picked[:], tabs[:].indirect(offsets[:]))
+        staged = raws.tile([P, S + H], U8, name="staged", tag="late", align_bytes=64)
+        nc.vector.tensor_copy(staged[:, :S].bitcast(I32), picked[:].bitcast(I32))
+        nc.vector.tensor_copy(
+            staged[:, S:].rearrange("p (b t m) -> p b m t", b=2, t=PACK),
+            w2s_raw[:].rearrange("p (b m t) -> p b m t", b=2, t=PACK),
+        )
+        for q in range(4):
+            nc.scalar.dma_start(
+                planes[32 * q : 32 * q + 4, :].bitcast(I32), staged[ROW0 + 4 * q : ROW0 + 4 * q + 4, :].bitcast(I32)
+            )
+        w1_raw1 = load_rows(w1[:, PASS : 2 * PASS], "late")
+        for half in range(2):
+            cols = slice(half * HALF // 16, (half + 1) * HALF // 16)
+            words = keep.tile([P, HALF], U32, name=f"vq{half}", align_bytes=64)
+            nc.vector.tensor_copy(words[:], tabw[:].bitcast(U32).indirect(offsets[:, cols]))
+            vq.append(words)
+
+        def on_scalar(raw):
+            return [("scalar", raw, 0, 32 * i, 32 * (i + 1)) for i in range(4)]
+
+        def on_vector(raw):
+            return [("vector", raw, 0, 64 * i, 64 * (i + 1)) for i in range(2)]
+
+        first = [("scalar", w1_lo, 0, 0, 64), ("vector", w1_hi, 64, 64, 108), ("scalar", w1_hi, 64, 108, 128)]
+        w1q = {0: quantise_weight("w1a", first, 2)}
+        w3_raw0 = load_rows(w3[0:PASS, :], "early")
+        w3q = {}
+
+        ysc = keep.tile([P, S], U8, name="ysc", align_bytes=64)
+        y_rows = out_0.rearrange("(p t) j -> p t j", t=PACK)
+        y_words = out_1[0].rearrange("p m t -> p (m t)").bitcast(I32)
+
+        xs, hq, ys = {}, {}, {}
+
+        def front(c, b):
+            j0, width = CHUNKS[c]
+            x = work.tile([P, 256, PACK], F32, name="x")
+            for u in range(width // UNIT):
+                half, lo = divmod(j0 + u * UNIT, HALF)
+                v_codes = vq[half][:, lo : lo + UNIT].bitcast(FP8X4)
+                v_scales = planes[:, j0 + u * UNIT : j0 + (u + 1) * UNIT]
+                pa = ps_a.tile([P, PACK, UNIT], F32, name="pa")
+                pb = ps_b.tile([P, PACK, UNIT], F32, name="pb")
+                for t in range(PACK):
+                    cols = slice(t * P, (t + 1) * P)
+                    nc.tensor.matmul_mx(
+                        out=pa[:, t, :], lhsT=w1q[b][0][:, cols].bitcast(FP8X4), lhsT_scale=w1q[b][1][:, cols],
+                        rhs=v_codes, rhs_scale=v_scales, start=True, stop=True,
+                    )
+                for t in range(PACK):
+                    c0 = b * PASS + t * P
+                    nc.tensor.matmul_mx(
+                        out=pb[:, t, :], lhsT=w2q[:, 2 * c0 : 2 * (c0 + P)].bitcast(FP4X4),
+                        lhsT_scale=planes[:, S + c0 : S + c0 + P],
+                        rhs=v_codes, rhs_scale=v_scales, start=True, stop=True,
+                    )
+                e = work.tile([P, UNIT, PACK], F32, name="e")
+                nc.scalar.activation(e[:], pa[:].rearrange("p t n -> p n t"), EXP)
+                nc.vector.scalar_tensor_tensor(
+                    x[:, u * UNIT : (u + 1) * UNIT, :], e[:], BIG, pb[:].rearrange("p t n -> p n t"),
+                    ALU.min, ALU.mult,
+                )
+            xs[c, b] = x
+
+        def back(c, b):
+            width = CHUNKS[c][1]
+            s = work.tile([P, 256, PACK], F32, name="s")
+            nc.scalar.activation(s[:, :width, :], xs[c, b][:, :width, :], EXP, scale=-1.0)
+            h = work.tile([P, 256, PACK], BF16, name="h", align_bytes=64)
+            nc.vector.tensor_tensor(
+                h[:, :width, :], s[:, :width, :], gt[:, b : b + 1, :].to_broadcast([P, width, PACK]), ALU.mult
+            )
+            codes = keep.tile([P, width], U32, name=f"hq{c}{b}", align_bytes=64)
+            scales = keep.tile([P, width], U8, name=f"hs{c}{b}", align_bytes=64)
+            nc.vector.quantize_mx(
+                out=codes[:].bitcast(FP8X4), scales=scales[:], in_=h[:, :width, :].rearrange("p n t -> p (n t)")
+            )
+            hq[c, b] = (codes, scales)
+
+        def scores(c):
+            j0, width = CHUNKS[c]
+            per_bank = PASS // width
+            y = keep.tile([P, PACK, width], F32, name=f"y{c}")
+            for t0 in range(0, PACK, per_bank):
+                py = ps_y.tile([P, per_bank, width], F32, name="py")
+                for t in range(t0, t0 + per_bank):
+                    cols = slice(t * P, (t + 1) * P)
+                    for b in range(2):
+                        nc.tensor.matmul_mx(
+                            out=py[:, t - t0, :], lhsT=w3q[b][0][:, cols].bitcast(FP8X4),
+                            lhsT_scale=w3q[b][1][:, cols], rhs=hq[c, b][0][:].bitcast(FP8X4),
+                            rhs_scale=hq[c, b][1][:], start=(b == 0), stop=(b == 1),
+                        )
+                nc.scalar.copy(y[:, t0 : t0 + per_bank, :], py[:])
+            nc.sync.dma_start(y_rows[:, :, j0 : j0 + width], y[:])
+            ys[c] = y
+
+        def planes_of(c):
+            j0, width = CHUNKS[c]
+            y = ys[c]
+            ybf = work.tile([P, 256 * PACK], BF16, name="ybf", align_bytes=64)
+            nc.vector.tensor_copy(
+                ybf[:, : width * PACK].rearrange("p (c i t) -> p c t i", i=4, t=PACK),
+                y[:].rearrange("p t (c i) -> p c t i", i=4),
+            )
+            codes = keep.tile([P, width], I32, name=f"yq{c}", align_bytes=64)
+            nc.vector.quantize_mx(
+                out=codes[:].bitcast(FP8X4), scales=ysc[:, j0 : j0 + width], in_=ybf[:, : width * PACK]
+            )
+            nc.sync.dma_start(y_words[:, j0 : j0 + width], codes[:])
+
+        front(0, 0)
+        front(1, 0)
+        back(0, 0)
+        w1q[1] = quantise_weight("w1b", on_scalar(w1_raw1), 1)
+        w3_raw1 = load_rows(w3[PASS : 2 * PASS, :], "late")
+        front(0, 1)
+        back(1, 0)
+        w3q[0] = quantise_weight("w3a", on_scalar(w3_raw0), 1)
+        front(1, 1)
+        back(0, 1)
+        w3q[1] = quantise_weight("w3b", on_vector(w3_raw1), 1)
+        front(2, 0)
+        back(1, 1)
+        scores(0)
+        front(2, 1)
+        back(2, 0)
+        scores(1)
+        planes_of(0)
+        front(3, 0)
+        back(2, 1)
+        front(4, 0)
+        back(3, 0)
+        scores(2)
+        planes_of(1)
+        front(3, 1)
+        back(4, 0)
+        front(4, 1)
+        back(3, 1)
+        scores(3)
+        back(4, 1)
+        scores(4)
+        planes_of(2)
+        planes_of(3)
+        planes_of(4)
+        for q in range(4):
+            nc.sync.dma_start(
+                out_2[0, 4 * q : 4 * q + 4, :].bitcast(I32), ysc[32 * q : 32 * q + 4, :].bitcast(I32)
+            )

@@ -34,7 +34,7 @@ def tile_list_survival_treatment_scores_kernel(
         lists = ctx.enter_context(tc.tile_pool(name="lists", bufs=1))
         keep = ctx.enter_context(tc.tile_pool(name="keep", bufs=1))
         raws = ctx.enter_context(tc.tile_pool(name="raws", bufs=1))
-        work = ctx.enter_context(tc.tile_pool(name="work", bufs=3))
+        work = ctx.enter_context(tc.tile_pool(name="work", bufs=4))
         ps_a = ctx.enter_context(tc.psum_pool(name="ps_a", bufs=3))
         ps_b = ctx.enter_context(tc.psum_pool(name="ps_b", bufs=3))
         ps_y = ctx.enter_context(tc.psum_pool(name="ps_y", bufs=2))
@@ -53,7 +53,7 @@ def tile_list_survival_treatment_scores_kernel(
         gt = keep.tile([P, 2, PACK], F32, name="gt")
         nc.scalar.dma_start(gt[:], g.rearrange("(b p t) -> p b t", t=PACK, p=P))
 
-        w2_raw = keep.tile([P, 2 * H], U8, name="w2_raw", align_bytes=64)
+        w2_raw = raws.tile([P, 2 * H], U8, name="w2_raw", tag="late", align_bytes=64)
         nc.sync.dma_start(w2_raw[:].bitcast(I32), w2_words[0].bitcast(I32))
         tabw = keep.tile([P, T], I32, name="tabw", align_bytes=64)
         nc.sync.dma_start(tabw[:], tab_words[0].rearrange("p t i -> p (t i)").bitcast(I32))
@@ -65,13 +65,13 @@ def tile_list_survival_treatment_scores_kernel(
 
         def quantise_weight(name, pieces, calls):
             grouped = keep.tile([P, PACK * PASS], BF16, name=name + "_bf", align_bytes=64)
-            dst = grouped[:].rearrange("p (t m j) -> p m j t", t=PACK, j=PACK)
-            for engine, raw, first, lo, hi in pieces:
-                src = raw[:].rearrange("p j (m t) -> p m j t", t=PACK)
+            dst = grouped[:].rearrange("p (u e m j) -> p u m j e", u=2, e=2, j=PACK)
+            for engine, raw, first, pairs, lo, hi in pieces:
+                src = raw[:].rearrange("p j (m u e) -> p u m j e", u=2, e=2)
                 if engine == "vector":
-                    nc.vector.tensor_copy(dst[:, lo:hi], src[:, lo - first : hi - first])
+                    nc.vector.tensor_copy(dst[:, pairs, lo:hi], src[:, pairs, lo - first : hi - first])
                 else:
-                    nc.scalar.copy(dst[:, lo:hi], src[:, lo - first : hi - first])
+                    nc.scalar.copy(dst[:, pairs, lo:hi], src[:, pairs, lo - first : hi - first])
             codes = keep.tile([P, PASS], U32, name=name + "_q", align_bytes=64)
             scales = keep.tile([P, PASS], U8, name=name + "_s", align_bytes=64)
             step = PASS // calls
@@ -88,25 +88,24 @@ def tile_list_survival_treatment_scores_kernel(
         nc.vector.memset(warm[:, 0:1], 0.0)
         nc.scalar.activation(warm[:, 1:2], warm[:, 0:1], EXP)
 
-        w2q = keep.tile([P, 2 * H], U8, name="w2q", align_bytes=64)
-        nc.vector.tensor_copy(
-            w2q[:].bitcast(U16).rearrange("p (b t m) -> p b m t", b=2, t=PACK),
-            w2_raw[:].bitcast(U16).rearrange("p (b m t) -> p b m t", b=2, t=PACK),
-        )
-
         vq = []
         picked = keep.tile([P, S], U8, name="picked", align_bytes=64)
         nc.vector.tensor_copy(picked[:], tabs[:].indirect(offsets[:]))
-        staged = raws.tile([P, S + H], U8, name="staged", tag="late", align_bytes=64)
+        staged = keep.tile([P, S + H], U8, name="staged", align_bytes=64)
         nc.vector.tensor_copy(staged[:, :S].bitcast(I32), picked[:].bitcast(I32))
         nc.vector.tensor_copy(
-            staged[:, S:].rearrange("p (b t m) -> p b m t", b=2, t=PACK),
-            w2s_raw[:].rearrange("p (b m t) -> p b m t", b=2, t=PACK),
+            staged[:, S:].rearrange("p (b t m) -> p b t m", b=2, t=PACK),
+            w2s_raw[:].rearrange("p (b m t) -> p b t m", b=2, t=PACK),
         )
         for q in range(4):
             nc.scalar.dma_start(
                 planes[32 * q : 32 * q + 4, :].bitcast(I32), staged[ROW0 + 4 * q : ROW0 + 4 * q + 4, :].bitcast(I32)
             )
+        w2q = keep.tile([P, 2 * H], U8, name="w2q", align_bytes=64)
+        nc.vector.tensor_copy(
+            w2q[:].bitcast(U16).rearrange("p (b t m) -> p b t m", b=2, t=PACK),
+            w2_raw[:].bitcast(U16).rearrange("p (b m t) -> p b t m", b=2, t=PACK),
+        )
         w1_raw1 = load_rows(w1[:, PASS : 2 * PASS], "late")
         for half in range(2):
             cols = slice(half * HALF // 16, (half + 1) * HALF // 16)
@@ -114,13 +113,20 @@ def tile_list_survival_treatment_scores_kernel(
             nc.vector.tensor_copy(words[:], tabw[:].bitcast(U32).indirect(offsets[:, cols]))
             vq.append(words)
 
-        def on_scalar(raw):
-            return [("scalar", raw, 0, 32 * i, 32 * (i + 1)) for i in range(4)]
+        both = slice(0, 2)
 
-        def on_vector(raw):
-            return [("vector", raw, 0, 64 * i, 64 * (i + 1)) for i in range(2)]
+        def shares(raw, quarters_on_vector):
+            quarters = [(slice(u, u + 1), lo, lo + 64) for u in range(2) for lo in (0, 64)]
+            on_vector = {0: [], 1: quarters[:1], 2: [(slice(0, 1), 0, P)], 4: [(slice(0, 1), 0, P), (slice(1, 2), 0, P)]}
+            return [("vector", raw, 0) + piece for piece in on_vector[quarters_on_vector]] + [
+                ("scalar", raw, 0) + piece for piece in quarters[quarters_on_vector:]
+            ]
 
-        first = [("scalar", w1_lo, 0, 0, 64), ("vector", w1_hi, 64, 64, 108), ("scalar", w1_hi, 64, 108, 128)]
+        first = [
+            ("scalar", w1_lo, 0, both, 0, 64),
+            ("vector", w1_hi, 64, both, 64, 108),
+            ("scalar", w1_hi, 64, both, 108, 128),
+        ]
         w1q = {0: quantise_weight("w1a", first, 2)}
         w3_raw0 = load_rows(w3[0:PASS, :], "early")
         w3q = {}
@@ -211,23 +217,23 @@ def tile_list_survival_treatment_scores_kernel(
         front(0, 0)
         front(1, 0)
         back(0, 0)
-        w1q[1] = quantise_weight("w1b", on_scalar(w1_raw1), 1)
+        w1q[1] = quantise_weight("w1b", shares(w1_raw1, 4), 1)
         w3_raw1 = load_rows(w3[PASS : 2 * PASS, :], "late")
         front(0, 1)
         back(1, 0)
-        w3q[0] = quantise_weight("w3a", on_scalar(w3_raw0), 1)
         front(1, 1)
         back(0, 1)
-        w3q[1] = quantise_weight("w3b", on_vector(w3_raw1), 1)
+        w3q[0] = quantise_weight("w3a", shares(w3_raw0, 1), 1)
         front(2, 0)
         back(1, 1)
-        scores(0)
+        w3q[1] = quantise_weight("w3b", shares(w3_raw1, 2), 1)
         front(2, 1)
         back(2, 0)
-        scores(1)
-        planes_of(0)
+        scores(0)
         front(3, 0)
         back(2, 1)
+        scores(1)
+        planes_of(0)
         front(4, 0)
         back(3, 0)
         scores(2)

@@ -19,11 +19,20 @@ EXP = mybir.ActivationFunctionType.Exp
 P = 128
 PACK = 4
 PASS = P * PACK
-UNIT = 128
-HALF = 512
-CHUNKS = [(0, 256), (256, 256), (512, 256), (768, 128), (896, 128)]
-BIG = 3.0e38
-ROW0 = P - 16
+PASSES = H // PASS
+SCALE_ROWS = PASS // 32
+ROW0 = P - SCALE_ROWS
+UNIT = PASS // PACK
+HALF = S // 2
+WIDE = 2 * UNIT
+CHUNKS = [(0, WIDE), (WIDE, WIDE), (2 * WIDE, WIDE), (3 * WIDE, UNIT), (3 * WIDE + UNIT, UNIT)]
+STEPS = [(0, 0), (1, 0), (0, 1), (1, 1), (2, 0), (2, 1), (3, 0), (4, 0), (3, 1), (4, 1)]
+LAST_WIDE = 2
+SURVIVE_LAG = 2
+QUANTISE_LAG = 3
+W3_STEP = 4
+SPLIT = 108
+FINITE = 3.0e38
 
 
 def tile_list_survival_treatment_scores_kernel(
@@ -35,6 +44,7 @@ def tile_list_survival_treatment_scores_kernel(
         keep = ctx.enter_context(tc.tile_pool(name="keep", bufs=1))
         raws = ctx.enter_context(tc.tile_pool(name="raws", bufs=1))
         work = ctx.enter_context(tc.tile_pool(name="work", bufs=4))
+        ahead = ctx.enter_context(tc.tile_pool(name="ahead", bufs=6))
         ps_a = ctx.enter_context(tc.psum_pool(name="ps_a", bufs=3))
         ps_b = ctx.enter_context(tc.psum_pool(name="ps_b", bufs=3))
         ps_y = ctx.enter_context(tc.psum_pool(name="ps_y", bufs=2))
@@ -50,8 +60,8 @@ def tile_list_survival_treatment_scores_kernel(
         nc.gpsimd.memset(w2s_raw[:ROW0, :].bitcast(I32), 0)
         planes = keep.tile([P, S + H], U8, name="planes", align_bytes=64)
         nc.gpsimd.memset(planes[:].bitcast(I32), 0)
-        gt = keep.tile([P, 2, PACK], F32, name="gt")
-        nc.scalar.dma_start(gt[:], g.rearrange("(b p t) -> p b t", t=PACK, p=P))
+        gt = keep.tile([P, PASSES, PACK], F32, name="gt")
+        nc.scalar.dma_start(gt[:], g.rearrange("(s p t) -> p s t", t=PACK, p=P))
 
         w2_raw = raws.tile([P, 2 * H], U8, name="w2_raw", tag="late", align_bytes=64)
         nc.sync.dma_start(w2_raw[:].bitcast(I32), w2_words[0].bitcast(I32))
@@ -63,124 +73,129 @@ def tile_list_survival_treatment_scores_kernel(
             nc.sync.dma_start(raw[:], rows.rearrange("(p j) c -> p j c", j=PACK))
             return raw
 
-        def quantise_weight(name, pieces, calls):
-            grouped = keep.tile([P, PACK * PASS], BF16, name=name + "_bf", align_bytes=64)
+        def deal(name, pieces):
+            grouped = keep.tile([P, PACK * PASS], BF16, name=name, align_bytes=64)
             dst = grouped[:].rearrange("p (u e m j) -> p u m j e", u=2, e=2, j=PACK)
-            for engine, raw, first, pairs, lo, hi in pieces:
+            for copy, raw, first, pairs, lo, hi in pieces:
                 src = raw[:].rearrange("p j (m u e) -> p u m j e", u=2, e=2)
-                if engine == "vector":
-                    nc.vector.tensor_copy(dst[:, pairs, lo:hi], src[:, pairs, lo - first : hi - first])
-                else:
-                    nc.scalar.copy(dst[:, pairs, lo:hi], src[:, pairs, lo - first : hi - first])
-            codes = keep.tile([P, PASS], U32, name=name + "_q", align_bytes=64)
-            scales = keep.tile([P, PASS], U8, name=name + "_s", align_bytes=64)
-            step = PASS // calls
-            for c0 in range(0, PASS, step):
+                copy(dst[:, pairs, lo:hi], src[:, pairs, lo - first : hi - first])
+            return grouped
+
+        def quantise(name, grouped, width, calls):
+            codes = keep.tile([P, width], U32, name=name + "_codes", align_bytes=64)
+            scales = keep.tile([P, width], U8, name=name + "_scales", align_bytes=64)
+            step = width // calls
+            for c0 in range(0, width, step):
                 nc.vector.quantize_mx(
-                    out=codes[:, c0 : c0 + step].bitcast(FP8X4), scales=scales[:, c0 : c0 + step],
+                    out=codes[:, c0 : c0 + step].bitcast(FP8X4),
+                    scales=scales[:, c0 : c0 + step],
                     in_=grouped[:, PACK * c0 : PACK * (c0 + step)],
                 )
             return codes, scales
 
         w1_lo = load_rows(w1[:, 0 : PASS // 2], "lo")
         w1_hi = load_rows(w1[:, PASS // 2 : PASS], "early")
-        warm = keep.tile([P, 2], F32, name="warm")
-        nc.vector.memset(warm[:, 0:1], 0.0)
-        nc.scalar.activation(warm[:, 1:2], warm[:, 0:1], EXP)
 
-        vq = []
         picked = keep.tile([P, S], U8, name="picked", align_bytes=64)
         nc.vector.tensor_copy(picked[:], tabs[:].indirect(offsets[:]))
         staged = keep.tile([P, S + H], U8, name="staged", align_bytes=64)
-        nc.vector.tensor_copy(staged[:, :S].bitcast(I32), picked[:].bitcast(I32))
         nc.vector.tensor_copy(
-            staged[:, S:].rearrange("p (b t m) -> p b t m", b=2, t=PACK),
-            w2s_raw[:].rearrange("p (b m t) -> p b t m", b=2, t=PACK),
+            staged[:, S:].rearrange("p (s t m) -> p s t m", s=PASSES, t=PACK),
+            w2s_raw[:].rearrange("p (s m t) -> p s t m", s=PASSES, t=PACK),
         )
+        nc.vector.tensor_copy(staged[:, :S].bitcast(I32), picked[:].bitcast(I32))
         for q in range(4):
             nc.scalar.dma_start(
-                planes[32 * q : 32 * q + 4, :].bitcast(I32), staged[ROW0 + 4 * q : ROW0 + 4 * q + 4, :].bitcast(I32)
+                planes[32 * q : 32 * q + 4, :].bitcast(I32),
+                staged[ROW0 + 4 * q : ROW0 + 4 * q + 4, :].bitcast(I32),
             )
         w2q = keep.tile([P, 2 * H], U8, name="w2q", align_bytes=64)
         nc.vector.tensor_copy(
-            w2q[:].bitcast(U16).rearrange("p (b t m) -> p b t m", b=2, t=PACK),
-            w2_raw[:].bitcast(U16).rearrange("p (b m t) -> p b t m", b=2, t=PACK),
+            w2q[:].bitcast(U16).rearrange("p (s t m) -> p s t m", s=PASSES, t=PACK),
+            w2_raw[:].bitcast(U16).rearrange("p (s m t) -> p s t m", s=PASSES, t=PACK),
         )
-        w1_raw1 = load_rows(w1[:, PASS : 2 * PASS], "late")
+        w1_second = load_rows(w1[:, PASS : 2 * PASS], "late")
+        vq = []
         for half in range(2):
-            cols = slice(half * HALF // 16, (half + 1) * HALF // 16)
             words = keep.tile([P, HALF], U32, name=f"vq{half}", align_bytes=64)
+            cols = slice(half * HALF // 16, (half + 1) * HALF // 16)
             nc.vector.tensor_copy(words[:], tabw[:].bitcast(U32).indirect(offsets[:, cols]))
             vq.append(words)
 
-        both = slice(0, 2)
+        both, even, odd = slice(0, 2), slice(0, 1), slice(1, 2)
+        on_vector, on_scalar = nc.vector.tensor_copy, nc.scalar.copy
+        w1_first_bf = deal(
+            "w1_first_bf",
+            [
+                (on_scalar, w1_lo, 0, both, 0, P // 2),
+                (on_vector, w1_hi, P // 2, both, P // 2, SPLIT),
+                (on_scalar, w1_hi, P // 2, both, SPLIT, P),
+            ],
+        )
+        w1q = [quantise("w1_first", w1_first_bf, PASS, 2)]
+        w3_raw = [load_rows(w3[0:PASS, :], "early")]
+        w1_second_bf = deal(
+            "w1_second_bf", [(on_vector, w1_second, 0, even, 0, P), (on_vector, w1_second, 0, odd, 0, P)]
+        )
+        w3_raw.append(load_rows(w3[PASS : 2 * PASS, :], "late"))
+        w3q = []
 
-        def shares(raw, quarters_on_vector):
-            quarters = [(slice(u, u + 1), lo, lo + 64) for u in range(2) for lo in (0, 64)]
-            on_vector = {0: [], 1: quarters[:1], 2: [(slice(0, 1), 0, P)], 4: [(slice(0, 1), 0, P), (slice(1, 2), 0, P)]}
-            return [("vector", raw, 0) + piece for piece in on_vector[quarters_on_vector]] + [
-                ("scalar", raw, 0) + piece for piece in quarters[quarters_on_vector:]
-            ]
-
-        first = [
-            ("scalar", w1_lo, 0, both, 0, 64),
-            ("vector", w1_hi, 64, both, 64, 108),
-            ("scalar", w1_hi, 64, both, 108, 128),
-        ]
-        w1q = {0: quantise_weight("w1a", first, 2)}
-        w3_raw0 = load_rows(w3[0:PASS, :], "early")
-        w3q = {}
-
-        ysc = keep.tile([P, S], U8, name="ysc", align_bytes=64)
+        y_scales = keep.tile([P, S], U8, name="y_scales", align_bytes=64)
+        y_codes = keep.tile([P, S], I32, name="y_codes", align_bytes=64)
         y_rows = out_0.rearrange("(p t) j -> p t j", t=PACK)
         y_words = out_1[0].rearrange("p m t -> p (m t)").bitcast(I32)
+        xs, hs, hq, ys, ybf = {}, {}, {}, {}, {}
 
-        xs, hq, ys = {}, {}, {}
-
-        def front(c, b):
+        def exposure(c, s):
             j0, width = CHUNKS[c]
-            x = work.tile([P, 256, PACK], F32, name="x")
-            for u in range(width // UNIT):
-                half, lo = divmod(j0 + u * UNIT, HALF)
+            x = ahead.tile([P, WIDE, PACK], F32, name="x")
+            for u0 in range(0, width, UNIT):
+                half, lo = divmod(j0 + u0, HALF)
                 v_codes = vq[half][:, lo : lo + UNIT].bitcast(FP8X4)
-                v_scales = planes[:, j0 + u * UNIT : j0 + (u + 1) * UNIT]
+                v_scales = planes[:, j0 + u0 : j0 + u0 + UNIT]
                 pa = ps_a.tile([P, PACK, UNIT], F32, name="pa")
                 pb = ps_b.tile([P, PACK, UNIT], F32, name="pb")
                 for t in range(PACK):
                     cols = slice(t * P, (t + 1) * P)
                     nc.tensor.matmul_mx(
-                        out=pa[:, t, :], lhsT=w1q[b][0][:, cols].bitcast(FP8X4), lhsT_scale=w1q[b][1][:, cols],
-                        rhs=v_codes, rhs_scale=v_scales, start=True, stop=True,
+                        out=pa[:, t, :],
+                        lhsT=w1q[s][0][:, cols].bitcast(FP8X4),
+                        lhsT_scale=w1q[s][1][:, cols],
+                        rhs=v_codes,
+                        rhs_scale=v_scales,
+                        start=True,
+                        stop=True,
                     )
                 for t in range(PACK):
-                    c0 = b * PASS + t * P
+                    c0 = s * PASS + t * P
                     nc.tensor.matmul_mx(
-                        out=pb[:, t, :], lhsT=w2q[:, 2 * c0 : 2 * (c0 + P)].bitcast(FP4X4),
+                        out=pb[:, t, :],
+                        lhsT=w2q[:, 2 * c0 : 2 * (c0 + P)].bitcast(FP4X4),
                         lhsT_scale=planes[:, S + c0 : S + c0 + P],
-                        rhs=v_codes, rhs_scale=v_scales, start=True, stop=True,
+                        rhs=v_codes,
+                        rhs_scale=v_scales,
+                        start=True,
+                        stop=True,
                     )
-                e = work.tile([P, UNIT, PACK], F32, name="e")
-                nc.scalar.activation(e[:], pa[:].rearrange("p t n -> p n t"), EXP)
+                hazard = ahead.tile([P, UNIT, PACK], F32, name="hazard")
+                nc.scalar.activation(hazard[:], pa[:].rearrange("p t n -> p n t"), EXP)
                 nc.vector.scalar_tensor_tensor(
-                    x[:, u * UNIT : (u + 1) * UNIT, :], e[:], BIG, pb[:].rearrange("p t n -> p n t"),
-                    ALU.min, ALU.mult,
+                    x[:, u0 : u0 + UNIT, :], hazard[:], FINITE, pb[:].rearrange("p t n -> p n t"), ALU.min, ALU.mult
                 )
-            xs[c, b] = x
+            xs[c, s] = x
 
-        def back(c, b):
+        def survive(c, s):
             width = CHUNKS[c][1]
-            s = work.tile([P, 256, PACK], F32, name="s")
-            nc.scalar.activation(s[:, :width, :], xs[c, b][:, :width, :], EXP, scale=-1.0)
-            h = work.tile([P, 256, PACK], BF16, name="h", align_bytes=64)
+            alive = work.tile([P, WIDE, PACK], F32, name="alive")
+            nc.scalar.activation(alive[:, :width, :], xs[c, s][:, :width, :], EXP, scale=-1.0)
+            h = work.tile([P, WIDE * PACK], BF16, name="h", align_bytes=64)
             nc.vector.tensor_tensor(
-                h[:, :width, :], s[:, :width, :], gt[:, b : b + 1, :].to_broadcast([P, width, PACK]), ALU.mult
+                h[:, : width * PACK].rearrange("p (n t) -> p n t", t=PACK),
+                alive[:, :width, :],
+                gt[:, s : s + 1, :].to_broadcast([P, width, PACK]),
+                ALU.mult,
             )
-            codes = keep.tile([P, width], U32, name=f"hq{c}{b}", align_bytes=64)
-            scales = keep.tile([P, width], U8, name=f"hs{c}{b}", align_bytes=64)
-            nc.vector.quantize_mx(
-                out=codes[:].bitcast(FP8X4), scales=scales[:], in_=h[:, :width, :].rearrange("p n t -> p (n t)")
-            )
-            hq[c, b] = (codes, scales)
+            hs[c, s] = h
 
         def scores(c):
             j0, width = CHUNKS[c]
@@ -190,65 +205,71 @@ def tile_list_survival_treatment_scores_kernel(
                 py = ps_y.tile([P, per_bank, width], F32, name="py")
                 for t in range(t0, t0 + per_bank):
                     cols = slice(t * P, (t + 1) * P)
-                    for b in range(2):
+                    for s in range(PASSES):
                         nc.tensor.matmul_mx(
-                            out=py[:, t - t0, :], lhsT=w3q[b][0][:, cols].bitcast(FP8X4),
-                            lhsT_scale=w3q[b][1][:, cols], rhs=hq[c, b][0][:].bitcast(FP8X4),
-                            rhs_scale=hq[c, b][1][:], start=(b == 0), stop=(b == 1),
+                            out=py[:, t - t0, :],
+                            lhsT=w3q[s][0][:, cols].bitcast(FP8X4),
+                            lhsT_scale=w3q[s][1][:, cols],
+                            rhs=hq[c, s][0][:].bitcast(FP8X4),
+                            rhs_scale=hq[c, s][1][:],
+                            start=(s == 0),
+                            stop=(s == PASSES - 1),
                         )
                 nc.scalar.copy(y[:, t0 : t0 + per_bank, :], py[:])
             nc.sync.dma_start(y_rows[:, :, j0 : j0 + width], y[:])
             ys[c] = y
 
-        def planes_of(c):
-            j0, width = CHUNKS[c]
-            y = ys[c]
-            ybf = work.tile([P, 256 * PACK], BF16, name="ybf", align_bytes=64)
-            nc.vector.tensor_copy(
-                ybf[:, : width * PACK].rearrange("p (c i t) -> p c t i", i=4, t=PACK),
-                y[:].rearrange("p t (c i) -> p c t i", i=4),
+        def round_scores(c):
+            width = CHUNKS[c][1]
+            rounded = work.tile([P, WIDE * PACK], BF16, name="rounded", align_bytes=64)
+            copy = on_scalar if c == LAST_WIDE else on_vector
+            copy(
+                rounded[:, : width * PACK].rearrange("p (n i t) -> p n t i", i=4, t=PACK),
+                ys[c][:].rearrange("p t (n i) -> p n t i", i=4),
             )
-            codes = keep.tile([P, width], I32, name=f"yq{c}", align_bytes=64)
-            nc.vector.quantize_mx(
-                out=codes[:].bitcast(FP8X4), scales=ysc[:, j0 : j0 + width], in_=ybf[:, : width * PACK]
-            )
-            nc.sync.dma_start(y_words[:, j0 : j0 + width], codes[:])
+            ybf[c] = rounded
 
-        front(0, 0)
-        front(1, 0)
-        back(0, 0)
-        w1q[1] = quantise_weight("w1b", shares(w1_raw1, 4), 1)
-        w3_raw1 = load_rows(w3[PASS : 2 * PASS, :], "late")
-        front(0, 1)
-        back(1, 0)
-        front(1, 1)
-        back(0, 1)
-        w3q[0] = quantise_weight("w3a", shares(w3_raw0, 1), 1)
-        front(2, 0)
-        back(1, 1)
-        w3q[1] = quantise_weight("w3b", shares(w3_raw1, 2), 1)
-        front(2, 1)
-        back(2, 0)
-        scores(0)
-        front(3, 0)
-        back(2, 1)
-        scores(1)
-        planes_of(0)
-        front(4, 0)
-        back(3, 0)
-        scores(2)
-        planes_of(1)
-        front(3, 1)
-        back(4, 0)
-        front(4, 1)
-        back(3, 1)
-        scores(3)
-        back(4, 1)
-        scores(4)
-        planes_of(2)
-        planes_of(3)
-        planes_of(4)
-        for q in range(4):
-            nc.sync.dma_start(
-                out_2[0, 4 * q : 4 * q + 4, :].bitcast(I32), ysc[32 * q : 32 * q + 4, :].bitcast(I32)
+        def quantise_scores(c):
+            j0, width = CHUNKS[c]
+            nc.vector.quantize_mx(
+                out=y_codes[:, j0 : j0 + width].bitcast(FP8X4),
+                scales=y_scales[:, j0 : j0 + width],
+                in_=ybf[c][:, : width * PACK],
+            )
+
+        for i in range(len(STEPS) + QUANTISE_LAG):
+            w3_pass = i - W3_STEP
+            if 0 <= w3_pass < PASSES:
+                raw = w3_raw[w3_pass]
+                w3_bf = deal(
+                    f"w3_bf{w3_pass}",
+                    [
+                        (on_vector, raw, 0, even, 0, P),
+                        (on_scalar, raw, 0, odd, 0, P // 2),
+                        (on_scalar, raw, 0, odd, P // 2, P),
+                    ],
+                )
+            if i < len(STEPS):
+                exposure(*STEPS[i])
+            if i == 0:
+                w1q.append(quantise("w1_second", w1_second_bf, PASS, 1))
+            if 0 <= w3_pass < PASSES:
+                w3q.append(quantise(f"w3_{w3_pass}", w3_bf, PASS, 1))
+            if 0 <= i - SURVIVE_LAG < len(STEPS):
+                survive(*STEPS[i - SURVIVE_LAG])
+            if i >= QUANTISE_LAG:
+                c, s = STEPS[i - QUANTISE_LAG]
+                hq[c, s] = quantise(f"h{c}{s}", hs[c, s], CHUNKS[c][1], 1)
+                if s == PASSES - 1:
+                    scores(c)
+        for c in range(len(CHUNKS) + 1):
+            if c < len(CHUNKS):
+                round_scores(c)
+            if c > 0:
+                quantise_scores(c - 1)
+        for j0 in range(0, S, WIDE):
+            nc.sync.dma_start(y_words[:, j0 : j0 + WIDE], y_codes[:, j0 : j0 + WIDE])
+        for q, queue in enumerate([nc.sync, nc.scalar, nc.sync, nc.scalar]):
+            queue.dma_start(
+                out_2[0, 4 * q : 4 * q + 4, :].bitcast(I32), y_scales[32 * q : 32 * q + 4, :].bitcast(I32)
             )

@@ -25,9 +25,18 @@ ROW0 = P - SCALE_ROWS
 UNIT = PASS // PACK
 HALF = S // 2
 WIDE = 2 * UNIT
-CHUNKS = [(0, WIDE), (WIDE, WIDE), (2 * WIDE, WIDE), (3 * WIDE, UNIT), (3 * WIDE + UNIT, UNIT)]
-STEPS = [(0, 0), (1, 0), (0, 1), (1, 1), (2, 0), (2, 1), (3, 0), (4, 0), (3, 1), (4, 1)]
-LAST_WIDE = 2
+GROUPS = [(0, WIDE), (WIDE, WIDE), (2 * WIDE, WIDE), (3 * WIDE, UNIT), (3 * WIDE + UNIT, UNIT)]
+STEPS = [
+    (0, WIDE, 0),
+    (WIDE, WIDE, 0),
+    (0, WIDE, 1),
+    (WIDE, WIDE, 1),
+    (2 * WIDE, WIDE, 0),
+    (2 * WIDE, WIDE, 1),
+    (3 * WIDE, WIDE, 0),
+    (3 * WIDE, UNIT, 1),
+    (3 * WIDE + UNIT, UNIT, 1),
+]
 SURVIVE_LAG = 2
 QUANTISE_LAG = 3
 W3_STEP = 4
@@ -75,10 +84,10 @@ def tile_list_survival_treatment_scores_kernel(
 
         def deal(name, pieces):
             grouped = keep.tile([P, PACK * PASS], BF16, name=name, align_bytes=64)
-            dst = grouped[:].rearrange("p (u e m j) -> p u m j e", u=2, e=2, j=PACK)
-            for copy, raw, first, pairs, lo, hi in pieces:
-                src = raw[:].rearrange("p j (m u e) -> p u m j e", u=2, e=2)
-                copy(dst[:, pairs, lo:hi], src[:, pairs, lo - first : hi - first])
+            dst = grouped[:].rearrange("p (t m j) -> p m t j", t=PACK, j=PACK)
+            for copy, raw, first, lo, hi in pieces:
+                src = raw[:].rearrange("p j (m t) -> p m t j", t=PACK)
+                copy(dst[:, lo:hi], src[:, lo - first : hi - first])
             return grouped
 
         def quantise(name, grouped, width, calls):
@@ -122,20 +131,19 @@ def tile_list_survival_treatment_scores_kernel(
             nc.vector.tensor_copy(words[:], tabw[:].bitcast(U32).indirect(offsets[:, cols]))
             vq.append(words)
 
-        both, even, odd = slice(0, 2), slice(0, 1), slice(1, 2)
         on_vector, on_scalar = nc.vector.tensor_copy, nc.scalar.copy
         w1_first_bf = deal(
             "w1_first_bf",
             [
-                (on_scalar, w1_lo, 0, both, 0, P // 2),
-                (on_vector, w1_hi, P // 2, both, P // 2, SPLIT),
-                (on_scalar, w1_hi, P // 2, both, SPLIT, P),
+                (on_scalar, w1_lo, 0, 0, P // 2),
+                (on_vector, w1_hi, P // 2, P // 2, SPLIT),
+                (on_scalar, w1_hi, P // 2, SPLIT, P),
             ],
         )
         w1q = [quantise("w1_first", w1_first_bf, PASS, 2)]
         w3_raw = [load_rows(w3[0:PASS, :], "early")]
         w1_second_bf = deal(
-            "w1_second_bf", [(on_vector, w1_second, 0, even, 0, P), (on_vector, w1_second, 0, odd, 0, P)]
+            "w1_second_bf", [(on_vector, w1_second, 0, 0, P // 2), (on_vector, w1_second, 0, P // 2, P)]
         )
         w3_raw.append(load_rows(w3[PASS : 2 * PASS, :], "late"))
         w3q = []
@@ -144,10 +152,13 @@ def tile_list_survival_treatment_scores_kernel(
         y_codes = keep.tile([P, S], I32, name="y_codes", align_bytes=64)
         y_rows = out_0.rearrange("(p t) j -> p t j", t=PACK)
         y_words = out_1[0].rearrange("p m t -> p (m t)").bitcast(I32)
-        xs, hs, hq, ys, ybf = {}, {}, {}, {}, {}
+        h = [keep.tile([P, S * PACK], BF16, name=f"h{s}", align_bytes=64) for s in range(PASSES)]
+        h_codes = [keep.tile([P, S], U32, name=f"h_codes{s}", align_bytes=64) for s in range(PASSES)]
+        h_scales = [keep.tile([P, S], U8, name=f"h_scales{s}", align_bytes=64) for s in range(PASSES)]
+        rounded = keep.tile([P, S * PACK], BF16, name="rounded", align_bytes=64)
+        xs, ys = {}, {}
 
-        def exposure(c, s):
-            j0, width = CHUNKS[c]
+        def exposure(j0, width, s):
             x = ahead.tile([P, WIDE, PACK], F32, name="x")
             for u0 in range(0, width, UNIT):
                 half, lo = divmod(j0 + u0, HALF)
@@ -155,17 +166,6 @@ def tile_list_survival_treatment_scores_kernel(
                 v_scales = planes[:, j0 + u0 : j0 + u0 + UNIT]
                 pa = ps_a.tile([P, PACK, UNIT], F32, name="pa")
                 pb = ps_b.tile([P, PACK, UNIT], F32, name="pb")
-                for t in range(PACK):
-                    cols = slice(t * P, (t + 1) * P)
-                    nc.tensor.matmul_mx(
-                        out=pa[:, t, :],
-                        lhsT=w1q[s][0][:, cols].bitcast(FP8X4),
-                        lhsT_scale=w1q[s][1][:, cols],
-                        rhs=v_codes,
-                        rhs_scale=v_scales,
-                        start=True,
-                        stop=True,
-                    )
                 for t in range(PACK):
                     c0 = s * PASS + t * P
                     nc.tensor.matmul_mx(
@@ -177,30 +177,43 @@ def tile_list_survival_treatment_scores_kernel(
                         start=True,
                         stop=True,
                     )
+                for t in range(PACK):
+                    cols = slice(t * P, (t + 1) * P)
+                    nc.tensor.matmul_mx(
+                        out=pa[:, t, :],
+                        lhsT=w1q[s][0][:, cols].bitcast(FP8X4),
+                        lhsT_scale=w1q[s][1][:, cols],
+                        rhs=v_codes,
+                        rhs_scale=v_scales,
+                        start=True,
+                        stop=True,
+                    )
                 hazard = ahead.tile([P, UNIT, PACK], F32, name="hazard")
                 nc.scalar.activation(hazard[:], pa[:].rearrange("p t n -> p n t"), EXP)
                 nc.vector.scalar_tensor_tensor(
-                    x[:, u0 : u0 + UNIT, :], hazard[:], FINITE, pb[:].rearrange("p t n -> p n t"), ALU.min, ALU.mult
+                    x[:, u0 : u0 + UNIT, :],
+                    hazard[:],
+                    FINITE,
+                    pb[:].rearrange("p t n -> p n t"),
+                    ALU.min,
+                    ALU.mult,
                 )
-            xs[c, s] = x
+            xs[j0, s] = x
 
-        def survive(c, s):
-            width = CHUNKS[c][1]
+        def survive(j0, width, s):
             alive = work.tile([P, WIDE, PACK], F32, name="alive")
-            nc.scalar.activation(alive[:, :width, :], xs[c, s][:, :width, :], EXP, scale=-1.0)
-            h = work.tile([P, WIDE * PACK], BF16, name="h", align_bytes=64)
+            nc.scalar.activation(alive[:, :width, :], xs[j0, s][:, :width, :], EXP, scale=-1.0)
             nc.vector.tensor_tensor(
-                h[:, : width * PACK].rearrange("p (n t) -> p n t", t=PACK),
+                h[s][:, j0 * PACK : (j0 + width) * PACK].rearrange("p (n t) -> p n t", t=PACK),
                 alive[:, :width, :],
                 gt[:, s : s + 1, :].to_broadcast([P, width, PACK]),
                 ALU.mult,
             )
-            hs[c, s] = h
 
-        def scores(c):
-            j0, width = CHUNKS[c]
+        def scores(j0, width):
             per_bank = PASS // width
-            y = keep.tile([P, PACK, width], F32, name=f"y{c}")
+            patients = slice(j0, j0 + width)
+            y = keep.tile([P, PACK, width], F32, name=f"y{j0}")
             for t0 in range(0, PACK, per_bank):
                 py = ps_y.tile([P, per_bank, width], F32, name="py")
                 for t in range(t0, t0 + per_bank):
@@ -210,31 +223,27 @@ def tile_list_survival_treatment_scores_kernel(
                             out=py[:, t - t0, :],
                             lhsT=w3q[s][0][:, cols].bitcast(FP8X4),
                             lhsT_scale=w3q[s][1][:, cols],
-                            rhs=hq[c, s][0][:].bitcast(FP8X4),
-                            rhs_scale=hq[c, s][1][:],
+                            rhs=h_codes[s][:, patients].bitcast(FP8X4),
+                            rhs_scale=h_scales[s][:, patients],
                             start=(s == 0),
                             stop=(s == PASSES - 1),
                         )
                 nc.scalar.copy(y[:, t0 : t0 + per_bank, :], py[:])
-            nc.sync.dma_start(y_rows[:, :, j0 : j0 + width], y[:])
-            ys[c] = y
+            nc.sync.dma_start(y_rows[:, :, patients], y[:])
+            ys[j0] = y
 
-        def round_scores(c):
-            width = CHUNKS[c][1]
-            rounded = work.tile([P, WIDE * PACK], BF16, name="rounded", align_bytes=64)
-            copy = on_scalar if c == LAST_WIDE else on_vector
-            copy(
-                rounded[:, : width * PACK].rearrange("p (n i t) -> p n t i", i=4, t=PACK),
-                ys[c][:].rearrange("p t (n i) -> p n t i", i=4),
-            )
-            ybf[c] = rounded
+        def round_scores(j0, width):
+            copy = on_scalar if (j0, width) == GROUPS[2] else on_vector
+            for lo in range(0, width, WIDE):
+                hi = min(lo + WIDE, width)
+                copy(
+                    rounded[:, (j0 + lo) * PACK : (j0 + hi) * PACK].rearrange("p (n t) -> p n t", t=PACK),
+                    ys[j0][:, :, lo:hi].rearrange("p t n -> p n t"),
+                )
 
-        def quantise_scores(c):
-            j0, width = CHUNKS[c]
+        def quantise_columns(values, codes, scales, lo, hi):
             nc.vector.quantize_mx(
-                out=y_codes[:, j0 : j0 + width].bitcast(FP8X4),
-                scales=y_scales[:, j0 : j0 + width],
-                in_=ybf[c][:, : width * PACK],
+                out=codes[:, lo:hi].bitcast(FP8X4), scales=scales[:, lo:hi], in_=values[:, lo * PACK : hi * PACK]
             )
 
         for i in range(len(STEPS) + QUANTISE_LAG):
@@ -244,9 +253,9 @@ def tile_list_survival_treatment_scores_kernel(
                 w3_bf = deal(
                     f"w3_bf{w3_pass}",
                     [
-                        (on_vector, raw, 0, even, 0, P),
-                        (on_scalar, raw, 0, odd, 0, P // 2),
-                        (on_scalar, raw, 0, odd, P // 2, P),
+                        (on_vector, raw, 0, 0, P // 2),
+                        (on_scalar, raw, 0, P // 2, 3 * P // 4),
+                        (on_scalar, raw, 0, 3 * P // 4, P),
                     ],
                 )
             if i < len(STEPS):
@@ -258,15 +267,19 @@ def tile_list_survival_treatment_scores_kernel(
             if 0 <= i - SURVIVE_LAG < len(STEPS):
                 survive(*STEPS[i - SURVIVE_LAG])
             if i >= QUANTISE_LAG:
-                c, s = STEPS[i - QUANTISE_LAG]
-                hq[c, s] = quantise(f"h{c}{s}", hs[c, s], CHUNKS[c][1], 1)
+                j0, width, s = STEPS[i - QUANTISE_LAG]
+                finished = [group for group in GROUPS if j0 < group[0] + group[1] <= j0 + width]
+                if finished:
+                    quantise_columns(h[s], h_codes[s], h_scales[s], finished[0][0], j0 + width)
                 if s == PASSES - 1:
-                    scores(c)
-        for c in range(len(CHUNKS) + 1):
-            if c < len(CHUNKS):
-                round_scores(c)
+                    for group in finished:
+                        scores(*group)
+        for c in range(len(GROUPS) + 1):
+            if c < len(GROUPS):
+                round_scores(*GROUPS[c])
             if c > 0:
-                quantise_scores(c - 1)
+                j0, width = GROUPS[c - 1]
+                quantise_columns(rounded, y_codes, y_scales, j0, j0 + width)
         for j0 in range(0, S, WIDE):
             nc.sync.dma_start(y_words[:, j0 : j0 + WIDE], y_codes[:, j0 : j0 + WIDE])
         for q, queue in enumerate([nc.sync, nc.scalar, nc.sync, nc.scalar]):

@@ -105,25 +105,34 @@ def tile_list_survival_treatment_scores_kernel(
         w1_lo = load_rows(w1[:, 0 : PASS // 2], "lo")
         w1_hi = load_rows(w1[:, PASS // 2 : PASS], "early")
 
-        picked = keep.tile([P, S], U8, name="picked", align_bytes=64)
-        nc.vector.tensor_copy(picked[:], tabs[:].indirect(offsets[:]))
-        staged = keep.tile([P, S + H], U8, name="staged", align_bytes=64)
-        nc.vector.tensor_copy(
-            staged[:, S:].rearrange("p (s t m) -> p s t m", s=PASSES, t=PACK),
+        def pick_scales(half):
+            picked = raws.tile([P, HALF], U8, name="picked", tag="picked", align_bytes=64)
+            cols = slice(half * HALF // 16, (half + 1) * HALF // 16)
+            nc.vector.tensor_copy(picked[:], tabs[:].indirect(offsets[:, cols]))
+            return picked
+
+        def to_plane_rows(queue, cols, source):
+            for q in range(4):
+                queue.dma_start(
+                    planes[32 * q : 32 * q + 4, cols].bitcast(I32),
+                    source[ROW0 + 4 * q : ROW0 + 4 * q + 4, :].bitcast(I32),
+                )
+
+        staged = keep.tile([P, H + HALF], U8, name="staged", align_bytes=64)
+        picked = pick_scales(0)
+        nc.gpsimd.tensor_copy(
+            staged[:, :H].rearrange("p (s t m) -> p s t m", s=PASSES, t=PACK),
             w2s_raw[:].rearrange("p (s m t) -> p s t m", s=PASSES, t=PACK),
         )
-        nc.vector.tensor_copy(staged[:, :S].bitcast(I32), picked[:].bitcast(I32))
-        for q in range(4):
-            nc.scalar.dma_start(
-                planes[32 * q : 32 * q + 4, :].bitcast(I32),
-                staged[ROW0 + 4 * q : ROW0 + 4 * q + 4, :].bitcast(I32),
-            )
+        nc.vector.tensor_copy(staged[:, H:].bitcast(I32), picked[:].bitcast(I32))
+        to_plane_rows(nc.scalar, slice(0, H + HALF), staged)
         w2q = keep.tile([P, 2 * H], U8, name="w2q", align_bytes=64)
         nc.vector.tensor_copy(
             w2q[:].bitcast(U16).rearrange("p (s t m) -> p s t m", s=PASSES, t=PACK),
             w2_raw[:].bitcast(U16).rearrange("p (s m t) -> p s t m", s=PASSES, t=PACK),
         )
         w1_second = load_rows(w1[:, PASS : 2 * PASS], "late")
+        to_plane_rows(nc.sync, slice(H + HALF, H + S), pick_scales(1))
         vq = []
         for half in range(2):
             words = keep.tile([P, HALF], U32, name=f"vq{half}", align_bytes=64)
@@ -163,7 +172,7 @@ def tile_list_survival_treatment_scores_kernel(
             for u0 in range(0, width, UNIT):
                 half, lo = divmod(j0 + u0, HALF)
                 v_codes = vq[half][:, lo : lo + UNIT].bitcast(FP8X4)
-                v_scales = planes[:, j0 + u0 : j0 + u0 + UNIT]
+                v_scales = planes[:, H + j0 + u0 : H + j0 + u0 + UNIT]
                 pa = ps_a.tile([P, PACK, UNIT], F32, name="pa")
                 pb = ps_b.tile([P, PACK, UNIT], F32, name="pb")
                 for t in range(PACK):
@@ -171,7 +180,7 @@ def tile_list_survival_treatment_scores_kernel(
                     nc.tensor.matmul_mx(
                         out=pb[:, t, :],
                         lhsT=w2q[:, 2 * c0 : 2 * (c0 + P)].bitcast(FP4X4),
-                        lhsT_scale=planes[:, S + c0 : S + c0 + P],
+                        lhsT_scale=planes[:, c0 : c0 + P],
                         rhs=v_codes,
                         rhs_scale=v_scales,
                         start=True,

@@ -1,6 +1,7 @@
 from contextlib import ExitStack
 
 import concourse.mybir as mybir
+from concourse.masks import make_identity
 
 K, T, S, H, N = 512, 4096, 1024, 1024, 512
 FLOPS = 2 * (2 * K * H * S + H * N * S)
@@ -26,20 +27,14 @@ UNIT = PASS // PACK
 HALF = S // 2
 WIDE = 2 * UNIT
 GROUPS = [(0, WIDE), (WIDE, WIDE), (2 * WIDE, WIDE), (3 * WIDE, UNIT), (3 * WIDE + UNIT, UNIT)]
-STEPS = [
-    (0, WIDE, 0),
-    (WIDE, WIDE, 0),
-    (0, WIDE, 1),
-    (WIDE, WIDE, 1),
-    (2 * WIDE, WIDE, 0),
-    (2 * WIDE, WIDE, 1),
-    (3 * WIDE, WIDE, 0),
-    (3 * WIDE, UNIT, 1),
-    (3 * WIDE + UNIT, UNIT, 1),
-]
-SURVIVE_LAG = 2
-QUANTISE_LAG = 3
-W3_STEP = 4
+STEPS = [(j0, WIDE, 0) for j0 in range(0, S, WIDE)] + [(j0, width, 1) for j0, width in GROUPS]
+UNITS = S // UNIT
+W3_AFTER = UNITS + 1
+SURVIVE_LAG = 1
+QUANTISE_LAG = 1
+ROUND_LAG = 7
+ON_SCALAR = (0, 2)
+SCALAR_LAG = 7
 SPLIT = 108
 FINITE = 3.0e38
 
@@ -54,23 +49,37 @@ def tile_list_survival_treatment_scores_kernel(
         raws = ctx.enter_context(tc.tile_pool(name="raws", bufs=1))
         work = ctx.enter_context(tc.tile_pool(name="work", bufs=4))
         ahead = ctx.enter_context(tc.tile_pool(name="ahead", bufs=6))
-        ps_a = ctx.enter_context(tc.psum_pool(name="ps_a", bufs=3))
-        ps_b = ctx.enter_context(tc.psum_pool(name="ps_b", bufs=3))
-        ps_y = ctx.enter_context(tc.psum_pool(name="ps_y", bufs=2))
+        banks = ctx.enter_context(tc.psum_pool(name="banks", bufs=1))
+
+        def bank(number, shape):
+            return banks.tile(shape, F32, name=f"bank{number}", tag=f"bank{number}")
 
         offsets = lists.tile([P, S // 16], U16, name="offsets")
         nc.sync.dma_start(offsets[:], offs)
 
         tabs = keep.tile([P, T], U8, name="tabs", align_bytes=64)
         nc.sync.dma_start(tabs[ROW0:, :].bitcast(I32), tab_scales[0].bitcast(I32))
-        nc.gpsimd.memset(tabs[:ROW0, :].bitcast(I32), 0)
+        nc.vector.memset(tabs[:ROW0, :].bitcast(I32), 0)
         w2s_raw = keep.tile([P, H], U8, name="w2s_raw", align_bytes=64)
         nc.sync.dma_start(w2s_raw[ROW0:, :].bitcast(I32), w2_scales[0].bitcast(I32))
-        nc.gpsimd.memset(w2s_raw[:ROW0, :].bitcast(I32), 0)
+        nc.vector.memset(w2s_raw[:ROW0, :].bitcast(I32), 0)
         planes = keep.tile([P, S + H], U8, name="planes", align_bytes=64)
-        nc.gpsimd.memset(planes[:].bitcast(I32), 0)
-        gt = keep.tile([P, PASSES, PACK], F32, name="gt")
-        nc.scalar.dma_start(gt[:], g.rearrange("(s p t) -> p s t", t=PACK, p=P))
+        nc.vector.memset(planes[:].bitcast(I32), 0)
+        g_columns = keep.tile([P, P], F32, name="g_columns")
+        nc.scalar.dma_start(
+            g_columns[:, : PASSES * PACK].rearrange("p (s t) -> p s t", t=PACK),
+            g.rearrange("(s p t) -> p s t", t=PACK, p=P),
+        )
+        nc.vector.memset(g_columns[:, PASSES * PACK :], 0.0)
+        identity = keep.tile([P, P], F32, name="identity")
+        make_identity(nc, identity[:])
+        g_turned = bank(5, [P, P])
+        nc.tensor.transpose(g_turned[:], g_columns[:], identity[:])
+        g_rows = keep.tile([P, P], F32, name="g_rows")
+        nc.vector.tensor_copy(g_rows[:], g_turned[:])
+        g_bank = bank(7, [P, P])
+        nc.tensor.transpose(g_bank[:], g_rows[:], identity[:])
+        gt = g_bank[:, : PASSES * PACK].rearrange("p (s t) -> p s t", t=PACK)
 
         w2_raw = raws.tile([P, 2 * H], U8, name="w2_raw", tag="late", align_bytes=64)
         nc.sync.dma_start(w2_raw[:].bitcast(I32), w2_words[0].bitcast(I32))
@@ -82,17 +91,18 @@ def tile_list_survival_treatment_scores_kernel(
             nc.sync.dma_start(raw[:], rows.rearrange("(p j) c -> p j c", j=PACK))
             return raw
 
-        def deal(name, pieces):
-            grouped = keep.tile([P, PACK * PASS], BF16, name=name, align_bytes=64)
-            dst = grouped[:].rearrange("p (t m j) -> p m t j", t=PACK, j=PACK)
+        def deal(grouped, pieces):
+            dst = grouped.rearrange("p (t m j) -> p m t j", t=PACK, j=PACK)
             for copy, raw, first, lo, hi in pieces:
                 src = raw[:].rearrange("p j (m t) -> p m t j", t=PACK)
                 copy(dst[:, lo:hi], src[:, lo - first : hi - first])
-            return grouped
 
-        def quantise(name, grouped, width, calls):
-            codes = keep.tile([P, width], U32, name=name + "_codes", align_bytes=64)
-            scales = keep.tile([P, width], U8, name=name + "_scales", align_bytes=64)
+        def on_gpsimd(dst, src):
+            nc.gpsimd.tensor_scalar(dst, src, 1.0, 0.0, ALU.mult, ALU.add)
+
+        def quantise(name, grouped, width, calls, codes_tag, scales_tag):
+            codes = raws.tile([P, width], U32, name=name + "_codes", tag=codes_tag, align_bytes=64)
+            scales = keep.tile([P, width], U8, name=name + "_scales", tag=scales_tag, align_bytes=64)
             step = width // calls
             for c0 in range(0, width, step):
                 nc.vector.quantize_mx(
@@ -120,7 +130,7 @@ def tile_list_survival_treatment_scores_kernel(
 
         staged = keep.tile([P, H + HALF], U8, name="staged", align_bytes=64)
         picked = pick_scales(0)
-        nc.gpsimd.tensor_copy(
+        nc.vector.tensor_copy(
             staged[:, :H].rearrange("p (s t m) -> p s t m", s=PASSES, t=PACK),
             w2s_raw[:].rearrange("p (s m t) -> p s t m", s=PASSES, t=PACK),
         )
@@ -141,20 +151,26 @@ def tile_list_survival_treatment_scores_kernel(
             vq.append(words)
 
         on_vector, on_scalar = nc.vector.tensor_copy, nc.scalar.copy
-        w1_first_bf = deal(
-            "w1_first_bf",
+        w1_first_bf = keep.tile([P, PACK * PASS], BF16, name="w1_first_bf", align_bytes=64)
+        deal(
+            w1_first_bf[:],
             [
                 (on_scalar, w1_lo, 0, 0, P // 2),
                 (on_vector, w1_hi, P // 2, P // 2, SPLIT),
                 (on_scalar, w1_hi, P // 2, SPLIT, P),
             ],
         )
-        w1q = [quantise("w1_first", w1_first_bf, PASS, 2)]
-        w3_raw = [load_rows(w3[0:PASS, :], "early")]
-        w1_second_bf = deal(
-            "w1_second_bf", [(on_vector, w1_second, 0, 0, P // 2), (on_vector, w1_second, 0, P // 2, P)]
-        )
-        w3_raw.append(load_rows(w3[PASS : 2 * PASS, :], "late"))
+        w1q = [quantise("w1_first", w1_first_bf, PASS, 2, "w1_first_codes", "w1_first_scales")]
+        w3_raw = [load_rows(w3[0:PASS, :], "lo"), load_rows(w3[PASS : 2 * PASS, :], "early")]
+        w1_second_bf = keep.tile([P, PACK * PASS], BF16, name="w1_second_bf", tag="rounded_w", align_bytes=64)
+        deal(w1_second_bf[:], [(on_vector, w1_second, 0, 0, P // 2), (on_vector, w1_second, 0, P // 2, P)])
+        w1q.append(quantise("w1_second", w1_second_bf, PASS, 1, "w1_second_codes", "w1_second_scales"))
+        w3_bf = [
+            keep.tile([P, PACK * PASS], BF16, name="w3_bf0", tag="rounded_w", align_bytes=64),
+            keep.tile([P, PACK * PASS], BF16, name="w3_bf1", tag="rounded_w1", align_bytes=64),
+        ]
+        for s in range(PASSES):
+            deal(w3_bf[s][:], [(on_gpsimd, w3_raw[s], 0, 0, P)])
         w3q = []
 
         y_scales = keep.tile([P, S], U8, name="y_scales", align_bytes=64)
@@ -162,7 +178,7 @@ def tile_list_survival_treatment_scores_kernel(
         y_rows = out_0.rearrange("(p t) j -> p t j", t=PACK)
         y_words = out_1[0].rearrange("p m t -> p (m t)").bitcast(I32)
         h = [keep.tile([P, S * PACK], BF16, name=f"h{s}", align_bytes=64) for s in range(PASSES)]
-        h_codes = [keep.tile([P, S], U32, name=f"h_codes{s}", align_bytes=64) for s in range(PASSES)]
+        h_codes = {1: keep.tile([P, S], U32, name="h_codes1", align_bytes=64)}
         h_scales = [keep.tile([P, S], U8, name=f"h_scales{s}", align_bytes=64) for s in range(PASSES)]
         rounded = keep.tile([P, S * PACK], BF16, name="rounded", align_bytes=64)
         xs, ys = {}, {}
@@ -173,8 +189,10 @@ def tile_list_survival_treatment_scores_kernel(
                 half, lo = divmod(j0 + u0, HALF)
                 v_codes = vq[half][:, lo : lo + UNIT].bitcast(FP8X4)
                 v_scales = planes[:, H + j0 + u0 : H + j0 + u0 + UNIT]
-                pa = ps_a.tile([P, PACK, UNIT], F32, name="pa")
-                pb = ps_b.tile([P, PACK, UNIT], F32, name="pb")
+                unit = s * UNITS + (j0 + u0) // UNIT
+                a_ring, b_ring = ([0, 1, 5], [2, 3, 4, 6]) if s == 0 else ([0, 1], [2, 3, 4])
+                pa = bank(a_ring[unit % len(a_ring)], [P, PACK, UNIT])
+                pb = bank(b_ring[unit % len(b_ring)], [P, PACK, UNIT])
                 for t in range(PACK):
                     c0 = s * PASS + t * P
                     nc.tensor.matmul_mx(
@@ -197,7 +215,10 @@ def tile_list_survival_treatment_scores_kernel(
                         start=True,
                         stop=True,
                     )
-                hazard = ahead.tile([P, UNIT, PACK], F32, name="hazard")
+                if unit in (W3_AFTER - 1, W3_AFTER):
+                    hazard = keep.tile([P, UNIT, PACK], F32, name="hazard", tag=f"after{unit}", align_bytes=64)
+                else:
+                    hazard = ahead.tile([P, UNIT, PACK], F32, name="hazard")
                 nc.scalar.activation(hazard[:], pa[:].rearrange("p t n -> p n t"), EXP)
                 nc.vector.scalar_tensor_tensor(
                     x[:, u0 : u0 + UNIT, :],
@@ -224,7 +245,7 @@ def tile_list_survival_treatment_scores_kernel(
             patients = slice(j0, j0 + width)
             y = keep.tile([P, PACK, width], F32, name=f"y{j0}")
             for t0 in range(0, PACK, per_bank):
-                py = ps_y.tile([P, per_bank, width], F32, name="py")
+                py = bank(5 + t0 // per_bank if width == WIDE else j0 // UNIT % 2, [P, per_bank, width])
                 for t in range(t0, t0 + per_bank):
                     cols = slice(t * P, (t + 1) * P)
                     for s in range(PASSES):
@@ -241,10 +262,10 @@ def tile_list_survival_treatment_scores_kernel(
             nc.sync.dma_start(y_rows[:, :, patients], y[:])
             ys[j0] = y
 
-        def round_scores(j0, width):
-            copy = on_scalar if (j0, width) == GROUPS[2] else on_vector
-            for lo in range(0, width, WIDE):
-                hi = min(lo + WIDE, width)
+        def round_scores(copy, j0, width):
+            piece = UNIT if (j0, width) in [GROUPS[c] for c in ON_SCALAR] else width
+            for lo in range(0, width, piece):
+                hi = lo + piece
                 copy(
                     rounded[:, (j0 + lo) * PACK : (j0 + hi) * PACK].rearrange("p (n t) -> p n t", t=PACK),
                     ys[j0][:, :, lo:hi].rearrange("p t n -> p n t"),
@@ -255,39 +276,27 @@ def tile_list_survival_treatment_scores_kernel(
                 out=codes[:, lo:hi].bitcast(FP8X4), scales=scales[:, lo:hi], in_=values[:, lo * PACK : hi * PACK]
             )
 
-        for i in range(len(STEPS) + QUANTISE_LAG):
-            w3_pass = i - W3_STEP
-            if 0 <= w3_pass < PASSES:
-                raw = w3_raw[w3_pass]
-                w3_bf = deal(
-                    f"w3_bf{w3_pass}",
-                    [
-                        (on_vector, raw, 0, 0, P // 2),
-                        (on_scalar, raw, 0, P // 2, 3 * P // 4),
-                        (on_scalar, raw, 0, 3 * P // 4, P),
-                    ],
-                )
+        first = len(STEPS) - len(GROUPS)
+        for i in range(len(STEPS) + ROUND_LAG + 1):
             if i < len(STEPS):
                 exposure(*STEPS[i])
-            if i == 0:
-                w1q.append(quantise("w1_second", w1_second_bf, PASS, 1))
-            if 0 <= w3_pass < PASSES:
-                w3q.append(quantise(f"w3_{w3_pass}", w3_bf, PASS, 1))
+            if i == W3_AFTER // 2:
+                w3q.append(quantise("w3_0", w3_bf[0], PASS, 1, "early", f"after{W3_AFTER}"))
+                w3q.append(quantise("w3_1", w3_bf[1], PASS, 1, "w3_1_codes", f"after{W3_AFTER - 1}"))
+                h_codes[0] = keep.tile([P, S], U32, name="h_codes0", tag="rounded_w1", align_bytes=64)
             if 0 <= i - SURVIVE_LAG < len(STEPS):
                 survive(*STEPS[i - SURVIVE_LAG])
-            if i >= QUANTISE_LAG:
-                j0, width, s = STEPS[i - QUANTISE_LAG]
-                finished = [group for group in GROUPS if j0 < group[0] + group[1] <= j0 + width]
-                if finished:
-                    quantise_columns(h[s], h_codes[s], h_scales[s], finished[0][0], j0 + width)
-                if s == PASSES - 1:
-                    for group in finished:
-                        scores(*group)
-        for c in range(len(GROUPS) + 1):
-            if c < len(GROUPS):
-                round_scores(*GROUPS[c])
-            if c > 0:
-                j0, width = GROUPS[c - 1]
+            if first <= i - QUANTISE_LAG < len(STEPS):
+                j0, width = STEPS[i - QUANTISE_LAG][:2]
+                for s in range(PASSES):
+                    quantise_columns(h[s], h_codes[s], h_scales[s], j0, j0 + width)
+                scores(j0, width)
+            if i - SCALAR_LAG - first in ON_SCALAR:
+                round_scores(on_scalar, *STEPS[i - SCALAR_LAG][:2])
+            if first <= i - ROUND_LAG < len(STEPS) and i - ROUND_LAG - first not in ON_SCALAR:
+                round_scores(on_vector, *STEPS[i - ROUND_LAG][:2])
+            if first <= i - ROUND_LAG - 1 < len(STEPS):
+                j0, width = STEPS[i - ROUND_LAG - 1][:2]
                 quantise_columns(rounded, y_codes, y_scales, j0, j0 + width)
         for j0 in range(0, S, WIDE):
             nc.sync.dma_start(y_words[:, j0 : j0 + WIDE], y_codes[:, j0 : j0 + WIDE])

@@ -32,6 +32,10 @@ UNITS = S // UNIT
 W3_AFTER = UNITS + 1
 SURVIVE_LAG = 1
 QUANTISE_LAG = 1
+SCORE_LAGS = (1, 1, 1, 1, 1)
+W1_AFTER = 2
+LEAD = 0
+CODE_STORES = (0, 512, 1024)
 ROUND_LAG = 7
 ON_SCALAR = (0, 2)
 SCALAR_LAG = 7
@@ -73,13 +77,8 @@ def tile_list_survival_treatment_scores_kernel(
         nc.vector.memset(g_columns[:, PASSES * PACK :], 0.0)
         identity = keep.tile([P, P], F32, name="identity")
         make_identity(nc, identity[:])
-        g_turned = bank(5, [P, P])
+        g_turned = bank(4, [P, P])
         nc.tensor.transpose(g_turned[:], g_columns[:], identity[:])
-        g_rows = keep.tile([P, P], F32, name="g_rows")
-        nc.vector.tensor_copy(g_rows[:], g_turned[:])
-        g_bank = bank(7, [P, P])
-        nc.tensor.transpose(g_bank[:], g_rows[:], identity[:])
-        gt = g_bank[:, : PASSES * PACK].rearrange("p (s t) -> p s t", t=PACK)
 
         w2_raw = raws.tile([P, 2 * H], U8, name="w2_raw", tag="late", align_bytes=64)
         nc.sync.dma_start(w2_raw[:].bitcast(I32), w2_words[0].bitcast(I32))
@@ -161,27 +160,21 @@ def tile_list_survival_treatment_scores_kernel(
             ],
         )
         w1q = [quantise("w1_first", w1_first_bf, PASS, 2, "w1_first_codes", "w1_first_scales")]
+        g_rows = keep.tile([P, P], F32, name="g_rows", tag="w1_first_bf", align_bytes=64)
+        nc.vector.tensor_copy(g_rows[:], g_turned[:])
         w3_raw = [load_rows(w3[0:PASS, :], "lo"), load_rows(w3[PASS : 2 * PASS, :], "early")]
-        w1_second_bf = keep.tile([P, PACK * PASS], BF16, name="w1_second_bf", tag="rounded_w", align_bytes=64)
-        deal(w1_second_bf[:], [(on_vector, w1_second, 0, 0, P // 2), (on_vector, w1_second, 0, P // 2, P)])
-        w1q.append(quantise("w1_second", w1_second_bf, PASS, 1, "w1_second_codes", "w1_second_scales"))
-        w3_bf = [
-            keep.tile([P, PACK * PASS], BF16, name="w3_bf0", tag="rounded_w", align_bytes=64),
-            keep.tile([P, PACK * PASS], BF16, name="w3_bf1", tag="rounded_w1", align_bytes=64),
-        ]
-        for s in range(PASSES):
-            deal(w3_bf[s][:], [(on_gpsimd, w3_raw[s], 0, 0, P)])
+        w1_second_bf = keep.tile([P, PACK * PASS], BF16, name="w1_second_bf", tag="rounded_w0", align_bytes=64)
+        deal(w1_second_bf[:], [(on_gpsimd, w1_second, 0, 0, P)])
+        w3_bf = []
         w3q = []
 
         y_scales = keep.tile([P, S], U8, name="y_scales", align_bytes=64)
         y_codes = keep.tile([P, S], I32, name="y_codes", align_bytes=64)
         y_rows = out_0.rearrange("(p t) j -> p t j", t=PACK)
         y_words = out_1[0].rearrange("p m t -> p (m t)").bitcast(I32)
-        h = [keep.tile([P, S * PACK], BF16, name=f"h{s}", align_bytes=64) for s in range(PASSES)]
-        h_codes = {1: keep.tile([P, S], U32, name="h_codes1", align_bytes=64)}
-        h_scales = [keep.tile([P, S], U8, name=f"h_scales{s}", align_bytes=64) for s in range(PASSES)]
-        rounded = keep.tile([P, S * PACK], BF16, name="rounded", align_bytes=64)
-        xs, ys = {}, {}
+        h, rounded = {}, {}
+        hq = {}
+        xs, ys, alives = {}, {}, {}
 
         def exposure(j0, width, s):
             x = ahead.tile([P, WIDE, PACK], F32, name="x")
@@ -190,7 +183,7 @@ def tile_list_survival_treatment_scores_kernel(
                 v_codes = vq[half][:, lo : lo + UNIT].bitcast(FP8X4)
                 v_scales = planes[:, H + j0 + u0 : H + j0 + u0 + UNIT]
                 unit = s * UNITS + (j0 + u0) // UNIT
-                a_ring, b_ring = ([0, 1, 5], [2, 3, 4, 6]) if s == 0 else ([0, 1], [2, 3, 4])
+                a_ring, b_ring = ([0, 1, 5, 6], [2, 3, 4]) if s == 0 else ([0, 1], [2, 3, 4])
                 pa = bank(a_ring[unit % len(a_ring)], [P, PACK, UNIT])
                 pb = bank(b_ring[unit % len(b_ring)], [P, PACK, UNIT])
                 for t in range(PACK):
@@ -215,7 +208,7 @@ def tile_list_survival_treatment_scores_kernel(
                         start=True,
                         stop=True,
                     )
-                if unit in (W3_AFTER - 1, W3_AFTER):
+                if unit in (W1_AFTER, W3_AFTER - 1, W3_AFTER):
                     hazard = keep.tile([P, UNIT, PACK], F32, name="hazard", tag=f"after{unit}", align_bytes=64)
                 else:
                     hazard = ahead.tile([P, UNIT, PACK], F32, name="hazard")
@@ -233,10 +226,16 @@ def tile_list_survival_treatment_scores_kernel(
         def survive(j0, width, s):
             alive = work.tile([P, WIDE, PACK], F32, name="alive")
             nc.scalar.activation(alive[:, :width, :], xs[j0, s][:, :width, :], EXP, scale=-1.0)
-            nc.vector.tensor_tensor(
-                h[s][:, j0 * PACK : (j0 + width) * PACK].rearrange("p (n t) -> p n t", t=PACK),
-                alive[:, :width, :],
-                gt[:, s : s + 1, :].to_broadcast([P, width, PACK]),
+            alives[j0, s] = alive
+
+        def weigh(engine, factors, tag, j0, width, s):
+            step0 = j0 if (j0, s) in alives else j0 - UNIT
+            if s == 0:
+                h[j0] = keep.tile([P, PASSES * width * PACK], BF16, name=f"h{j0}", tag=tag, align_bytes=64)
+            engine.tensor_tensor(
+                h[j0][:, s * width * PACK : (s + 1) * width * PACK].rearrange("p (n t) -> p n t", t=PACK),
+                alives[step0, s][:, j0 - step0 : j0 - step0 + width, :],
+                factors[:, s * PACK : (s + 1) * PACK].unsqueeze(1).to_broadcast([P, width, PACK]),
                 ALU.mult,
             )
 
@@ -253,8 +252,8 @@ def tile_list_survival_treatment_scores_kernel(
                             out=py[:, t - t0, :],
                             lhsT=w3q[s][0][:, cols].bitcast(FP8X4),
                             lhsT_scale=w3q[s][1][:, cols],
-                            rhs=h_codes[s][:, patients].bitcast(FP8X4),
-                            rhs_scale=h_scales[s][:, patients],
+                            rhs=hq[j0][0][:, s * width : (s + 1) * width].bitcast(FP8X4),
+                            rhs_scale=hq[j0][1][:, s * width : (s + 1) * width],
                             start=(s == 0),
                             stop=(s == PASSES - 1),
                         )
@@ -262,44 +261,62 @@ def tile_list_survival_treatment_scores_kernel(
             nc.sync.dma_start(y_rows[:, :, patients], y[:])
             ys[j0] = y
 
-        def round_scores(copy, j0, width):
-            piece = UNIT if (j0, width) in [GROUPS[c] for c in ON_SCALAR] else width
+        def round_scores(copy, piece, tag, j0, width):
+            rounded[j0] = keep.tile([P, width * PACK], BF16, name=f"rounded{j0}", tag=tag, align_bytes=64)
             for lo in range(0, width, piece):
-                hi = lo + piece
                 copy(
-                    rounded[:, (j0 + lo) * PACK : (j0 + hi) * PACK].rearrange("p (n t) -> p n t", t=PACK),
-                    ys[j0][:, :, lo:hi].rearrange("p t n -> p n t"),
+                    rounded[j0][:, lo * PACK : (lo + piece) * PACK].rearrange("p (n t) -> p n t", t=PACK),
+                    ys[j0][:, :, lo : lo + piece].rearrange("p t n -> p n t"),
                 )
 
-        def quantise_columns(values, codes, scales, lo, hi):
-            nc.vector.quantize_mx(
-                out=codes[:, lo:hi].bitcast(FP8X4), scales=scales[:, lo:hi], in_=values[:, lo * PACK : hi * PACK]
-            )
+        def quantise_columns(values, codes, scales, j0, width):
+            cols = slice(j0, j0 + width)
+            nc.vector.quantize_mx(out=codes[:, cols].bitcast(FP8X4), scales=scales[:, cols], in_=values[:])
 
         first = len(STEPS) - len(GROUPS)
-        for i in range(len(STEPS) + ROUND_LAG + 1):
-            if i < len(STEPS):
+        for i in range(len(STEPS) + 2):
+            if i < len(STEPS) - 1:
                 exposure(*STEPS[i])
+            if i == len(STEPS) - 1 - LEAD:
+                exposure(*STEPS[-1])
+            if i == W1_AFTER // 2:
+                w1q.append(quantise("w1_second", w1_second_bf, PASS, 1, "w1_second_codes", f"after{W1_AFTER}"))
+                for s in range(PASSES):
+                    w3_bf.append(keep.tile([P, PACK * PASS], BF16, name=f"w3_bf{s}", tag=f"rounded_w{s}", align_bytes=64))
+                    deal(w3_bf[s][:], [(on_gpsimd, w3_raw[s], 0, 0, P)])
             if i == W3_AFTER // 2:
                 w3q.append(quantise("w3_0", w3_bf[0], PASS, 1, "early", f"after{W3_AFTER}"))
                 w3q.append(quantise("w3_1", w3_bf[1], PASS, 1, "w3_1_codes", f"after{W3_AFTER - 1}"))
-                h_codes[0] = keep.tile([P, S], U32, name="h_codes0", tag="rounded_w1", align_bytes=64)
-            if 0 <= i - SURVIVE_LAG < len(STEPS):
-                survive(*STEPS[i - SURVIVE_LAG])
-            if first <= i - QUANTISE_LAG < len(STEPS):
-                j0, width = STEPS[i - QUANTISE_LAG][:2]
-                for s in range(PASSES):
-                    quantise_columns(h[s], h_codes[s], h_scales[s], j0, j0 + width)
-                scores(j0, width)
-            if i - SCALAR_LAG - first in ON_SCALAR:
-                round_scores(on_scalar, *STEPS[i - SCALAR_LAG][:2])
-            if first <= i - ROUND_LAG < len(STEPS) and i - ROUND_LAG - first not in ON_SCALAR:
-                round_scores(on_vector, *STEPS[i - ROUND_LAG][:2])
-            if first <= i - ROUND_LAG - 1 < len(STEPS):
-                j0, width = STEPS[i - ROUND_LAG - 1][:2]
-                quantise_columns(rounded, y_codes, y_scales, j0, j0 + width)
-        for j0 in range(0, S, WIDE):
-            nc.sync.dma_start(y_words[:, j0 : j0 + WIDE], y_codes[:, j0 : j0 + WIDE])
+            if i == 0:
+                g_bank = bank(7, [P, P])
+                nc.tensor.transpose(g_bank[:], g_rows[:], identity[:])
+            if 0 <= i - 1 < len(STEPS):
+                j0, width, s = STEPS[i - 1]
+                survive(j0, width, s)
+                if i != first:
+                    weigh(nc.vector, g_bank, f"h{j0}", j0, width, s)
+                else:
+                    weigh(nc.gpsimd, g_columns, "rounded_w0", *GROUPS[-2], 0)
+                if s == 1:
+                    hq[j0] = quantise(f"h{j0}", h[j0], PASSES * width, 1, f"h{j0}_codes", f"h{j0}_scales")
+                if i - 1 == first:
+                    weigh(nc.gpsimd, g_columns, f"h{j0}", *GROUPS[-1], 0)
+                if i - 1 == first + 1:
+                    round_scores(on_gpsimd, WIDE, f"h{j0}", *GROUPS[0])
+            for c, group in enumerate(GROUPS):
+                if i == first + c + SCORE_LAGS[c] and group[0] not in ys:
+                    scores(*group)
+        round_scores(on_vector, WIDE, "rounded1", *GROUPS[1])
+        quantise_columns(rounded[0], y_codes, y_scales, *GROUPS[0])
+        round_scores(on_scalar, UNIT, "rounded2", *GROUPS[2])
+        quantise_columns(rounded[WIDE], y_codes, y_scales, *GROUPS[1])
+        round_scores(on_vector, UNIT, "rounded3", *GROUPS[3])
+        quantise_columns(rounded[2 * WIDE], y_codes, y_scales, *GROUPS[2])
+        round_scores(on_vector, UNIT, "rounded4", *GROUPS[4])
+        for j0, width in GROUPS[3:]:
+            quantise_columns(rounded[j0], y_codes, y_scales, j0, width)
+        for lo, hi in zip(CODE_STORES, CODE_STORES[1:]):
+            nc.sync.dma_start(y_words[:, lo:hi], y_codes[:, lo:hi])
         for q, queue in enumerate([nc.sync, nc.scalar, nc.sync, nc.scalar]):
             queue.dma_start(
                 out_2[0, 4 * q : 4 * q + 4, :].bitcast(I32), y_scales[32 * q : 32 * q + 4, :].bitcast(I32)

@@ -24,23 +24,20 @@ PASSES = H // PASS
 SCALE_ROWS = PASS // 32
 ROW0 = P - SCALE_ROWS
 UNIT = PASS // PACK
+UNITS = S // UNIT
 HALF = S // 2
 WIDE = 2 * UNIT
 GROUPS = [(0, WIDE), (WIDE, WIDE), (2 * WIDE, WIDE), (3 * WIDE, UNIT), (3 * WIDE + UNIT, UNIT)]
-STEPS = [(j0, WIDE, 0) for j0 in range(0, S, WIDE)] + [(j0, width, 1) for j0, width in GROUPS]
-UNITS = S // UNIT
-W3_AFTER = UNITS + 1
-SURVIVE_LAG = 1
-QUANTISE_LAG = 1
-SCORE_LAGS = (1, 1, 1, 1, 1)
-W1_AFTER = 2
-LEAD = 0
-CODE_STORES = (0, 512, 1024)
-ROUND_LAG = 7
-ON_SCALAR = (0, 2)
-SCALAR_LAG = 7
+ON_VECTOR = 2
 SPLIT = 108
+W1_AFTER = 1
+W3_AFTER = UNITS + 1
 FINITE = 3.0e38
+
+A_BANKS, A_BANKS_LATE, A_LATE_FROM = (0, 1, 5, 6), (0, 1), UNITS + 4
+B_BANKS = (2, 3, 4)
+Y_BANKS = ((5, 6), (5, 6), (0, 1), (2,), (3,))
+G_BANK, G_TURN_BANK = 7, 4
 
 
 def tile_list_survival_treatment_scores_kernel(
@@ -50,7 +47,6 @@ def tile_list_survival_treatment_scores_kernel(
     with ExitStack() as ctx:
         lists = ctx.enter_context(tc.tile_pool(name="lists", bufs=1))
         keep = ctx.enter_context(tc.tile_pool(name="keep", bufs=1))
-        raws = ctx.enter_context(tc.tile_pool(name="raws", bufs=1))
         work = ctx.enter_context(tc.tile_pool(name="work", bufs=4))
         ahead = ctx.enter_context(tc.tile_pool(name="ahead", bufs=6))
         banks = ctx.enter_context(tc.psum_pool(name="banks", bufs=1))
@@ -58,17 +54,26 @@ def tile_list_survival_treatment_scores_kernel(
         def bank(number, shape):
             return banks.tile(shape, F32, name=f"bank{number}", tag=f"bank{number}")
 
+        def held(shape, dtype, name, tag=None):
+            return keep.tile(shape, dtype, name=name, tag=tag or name, align_bytes=64)
+
+        on_vector, on_scalar = nc.vector.tensor_copy, nc.scalar.copy
+
+        def on_gpsimd(dst, src):
+            nc.gpsimd.tensor_scalar(dst, src, 1.0, 0.0, ALU.mult, ALU.add)
+
         offsets = lists.tile([P, S // 16], U16, name="offsets")
         nc.sync.dma_start(offsets[:], offs)
 
-        tabs = keep.tile([P, T], U8, name="tabs", align_bytes=64)
+        tabs = held([P, T], U8, "tabs", "w1_second")
         nc.sync.dma_start(tabs[ROW0:, :].bitcast(I32), tab_scales[0].bitcast(I32))
         nc.vector.memset(tabs[:ROW0, :].bitcast(I32), 0)
-        w2s_raw = keep.tile([P, H], U8, name="w2s_raw", align_bytes=64)
+        w2s_raw = held([P, H], U8, "w2s_raw")
         nc.sync.dma_start(w2s_raw[ROW0:, :].bitcast(I32), w2_scales[0].bitcast(I32))
         nc.vector.memset(w2s_raw[:ROW0, :].bitcast(I32), 0)
-        planes = keep.tile([P, S + H], U8, name="planes", align_bytes=64)
+        planes = held([P, H + S], U8, "planes")
         nc.vector.memset(planes[:].bitcast(I32), 0)
+
         g_columns = keep.tile([P, P], F32, name="g_columns")
         nc.scalar.dma_start(
             g_columns[:, : PASSES * PACK].rearrange("p (s t) -> p s t", t=PACK),
@@ -77,104 +82,107 @@ def tile_list_survival_treatment_scores_kernel(
         nc.vector.memset(g_columns[:, PASSES * PACK :], 0.0)
         identity = keep.tile([P, P], F32, name="identity")
         make_identity(nc, identity[:])
-        g_turned = bank(4, [P, P])
+        g_turned = bank(G_TURN_BANK, [P, P])
         nc.tensor.transpose(g_turned[:], g_columns[:], identity[:])
 
-        w2_raw = raws.tile([P, 2 * H], U8, name="w2_raw", tag="late", align_bytes=64)
-        nc.sync.dma_start(w2_raw[:].bitcast(I32), w2_words[0].bitcast(I32))
-        tabw = keep.tile([P, T], I32, name="tabw", align_bytes=64)
-        nc.sync.dma_start(tabw[:], tab_words[0].rearrange("p t i -> p (t i)").bitcast(I32))
-
-        def load_rows(rows, tag):
-            raw = raws.tile([P, PACK, rows.shape[1]], F32, name="raw", tag=tag, align_bytes=64)
-            nc.sync.dma_start(raw[:], rows.rearrange("(p j) c -> p j c", j=PACK))
+        def load_w2(s, tag):
+            raw = held([P, 2 * PASS], U8, f"w2_raw{s}", tag)
+            nc.sync.dma_start(raw[:].bitcast(I32), w2_words[0][:, 2 * s * PASS : 2 * (s + 1) * PASS].bitcast(I32))
             return raw
 
-        def deal(grouped, pieces):
-            dst = grouped.rearrange("p (t m j) -> p m t j", t=PACK, j=PACK)
-            for copy, raw, first, lo, hi in pieces:
-                src = raw[:].rearrange("p j (m t) -> p m t j", t=PACK)
-                copy(dst[:, lo:hi], src[:, lo - first : hi - first])
+        def deal_w2(raw, name, tag):
+            words = held([P, 2 * PASS], U8, name, tag)
+            nc.vector.tensor_copy(
+                words[:].bitcast(U16).rearrange("p (t m) -> p t m", t=PACK),
+                raw[:].bitcast(U16).rearrange("p (m t) -> p t m", t=PACK),
+            )
+            return words
 
-        def on_gpsimd(dst, src):
-            nc.gpsimd.tensor_scalar(dst, src, 1.0, 0.0, ALU.mult, ALU.add)
+        def by_partition(rows):
+            return rows.rearrange("(p j) c -> p j c", j=PACK)
 
-        def quantise(name, grouped, width, calls, codes_tag, scales_tag):
-            codes = raws.tile([P, width], U32, name=name + "_codes", tag=codes_tag, align_bytes=64)
-            scales = keep.tile([P, width], U8, name=name + "_scales", tag=scales_tag, align_bytes=64)
+        def load_rows(rows, name, tag):
+            raw = held([P, PACK, rows.shape[1]], F32, name, tag)
+            nc.sync.dma_start(raw[:], by_partition(rows))
+            return raw
+
+        def deal(copy, grouped, raw, first, lo, hi):
+            dst = grouped[:].rearrange("p (t m j) -> p m t j", t=PACK, j=PACK)
+            src = raw.rearrange("p j (m t) -> p m t j", t=PACK)
+            copy(dst[:, lo:hi], src[:, lo - first : hi - first])
+
+        def quantise(name, values, width, calls=1, codes_tag=None, scales_tag=None):
+            codes = held([P, width], U32, name + "_codes", codes_tag)
+            scales = held([P, width], U8, name + "_scales", scales_tag)
             step = width // calls
             for c0 in range(0, width, step):
                 nc.vector.quantize_mx(
                     out=codes[:, c0 : c0 + step].bitcast(FP8X4),
                     scales=scales[:, c0 : c0 + step],
-                    in_=grouped[:, PACK * c0 : PACK * (c0 + step)],
+                    in_=values[:, PACK * c0 : PACK * (c0 + step)],
                 )
             return codes, scales
 
-        w1_lo = load_rows(w1[:, 0 : PASS // 2], "lo")
-        w1_hi = load_rows(w1[:, PASS // 2 : PASS], "early")
-
         def pick_scales(half):
-            picked = raws.tile([P, HALF], U8, name="picked", tag="picked", align_bytes=64)
+            picked = held([P, HALF], U8, "picked")
             cols = slice(half * HALF // 16, (half + 1) * HALF // 16)
             nc.vector.tensor_copy(picked[:], tabs[:].indirect(offsets[:, cols]))
             return picked
 
-        def to_plane_rows(queue, cols, source):
+        def to_plane_rows(cols, source):
             for q in range(4):
-                queue.dma_start(
+                nc.sync.dma_start(
                     planes[32 * q : 32 * q + 4, cols].bitcast(I32),
                     source[ROW0 + 4 * q : ROW0 + 4 * q + 4, :].bitcast(I32),
                 )
 
-        staged = keep.tile([P, H + HALF], U8, name="staged", align_bytes=64)
+        w2_first = load_w2(0, "w1_hi")
+        tabw = held([P, T], I32, "tabw")
+        nc.sync.dma_start(tabw[:], tab_words[0].rearrange("p t i -> p (t i)").bitcast(I32))
+        w1_lo = load_rows(w1[:, 0 : PASS // 2], "w1_lo", "w1_lo")
+
+        staged = held([P, H + HALF], U8, "staged")
         picked = pick_scales(0)
         nc.vector.tensor_copy(
             staged[:, :H].rearrange("p (s t m) -> p s t m", s=PASSES, t=PACK),
             w2s_raw[:].rearrange("p (s m t) -> p s t m", s=PASSES, t=PACK),
         )
         nc.vector.tensor_copy(staged[:, H:].bitcast(I32), picked[:].bitcast(I32))
-        to_plane_rows(nc.scalar, slice(0, H + HALF), staged)
-        w2q = keep.tile([P, 2 * H], U8, name="w2q", align_bytes=64)
-        nc.vector.tensor_copy(
-            w2q[:].bitcast(U16).rearrange("p (s t m) -> p s t m", s=PASSES, t=PACK),
-            w2_raw[:].bitcast(U16).rearrange("p (s m t) -> p s t m", s=PASSES, t=PACK),
-        )
-        w1_second = load_rows(w1[:, PASS : 2 * PASS], "late")
-        to_plane_rows(nc.sync, slice(H + HALF, H + S), pick_scales(1))
+        to_plane_rows(slice(0, H + HALF), staged)
+        w2q = [deal_w2(w2_first, "w2q0", None)]
+        w1_hi = load_rows(w1[:, PASS // 2 : PASS], "w1_hi", "w1_hi")
+        picked = pick_scales(1)
+        w1_second = held([P, 2, PACK, PASS // 2], F32, "w1_second")
+        for half in range(2):
+            c0 = PASS + half * PASS // 2
+            nc.sync.dma_start(w1_second[:, half], by_partition(w1[:, c0 : c0 + PASS // 2]))
+        to_plane_rows(slice(H + HALF, H + S), picked)
+        w2_second = load_w2(1, "staged")
+
         vq = []
         for half in range(2):
-            words = keep.tile([P, HALF], U32, name=f"vq{half}", align_bytes=64)
+            words = held([P, HALF], U32, f"vq{half}")
             cols = slice(half * HALF // 16, (half + 1) * HALF // 16)
             nc.vector.tensor_copy(words[:], tabw[:].bitcast(U32).indirect(offsets[:, cols]))
             vq.append(words)
 
-        on_vector, on_scalar = nc.vector.tensor_copy, nc.scalar.copy
-        w1_first_bf = keep.tile([P, PACK * PASS], BF16, name="w1_first_bf", align_bytes=64)
-        deal(
-            w1_first_bf[:],
-            [
-                (on_scalar, w1_lo, 0, 0, P // 2),
-                (on_vector, w1_hi, P // 2, P // 2, SPLIT),
-                (on_scalar, w1_hi, P // 2, SPLIT, P),
-            ],
-        )
-        w1q = [quantise("w1_first", w1_first_bf, PASS, 2, "w1_first_codes", "w1_first_scales")]
-        g_rows = keep.tile([P, P], F32, name="g_rows", tag="w1_first_bf", align_bytes=64)
+        w1_first_bf = held([P, PACK * PASS], BF16, "w1_first_bf")
+        deal(on_scalar, w1_first_bf, w1_lo[:], 0, 0, P // 2)
+        deal(on_vector, w1_first_bf, w1_hi[:], P // 2, P // 2, SPLIT)
+        deal(on_scalar, w1_first_bf, w1_hi[:], P // 2, SPLIT, P)
+        w1q = [quantise("w1_first", w1_first_bf, PASS, calls=2)]
+        g_rows = held([P, P], F32, "g_rows")
         nc.vector.tensor_copy(g_rows[:], g_turned[:])
-        w3_raw = [load_rows(w3[0:PASS, :], "lo"), load_rows(w3[PASS : 2 * PASS, :], "early")]
-        w1_second_bf = keep.tile([P, PACK * PASS], BF16, name="w1_second_bf", tag="rounded_w0", align_bytes=64)
-        deal(w1_second_bf[:], [(on_gpsimd, w1_second, 0, 0, P)])
-        w3_bf = []
-        w3q = []
+        w3_raw = [load_rows(w3[0:PASS, :], "w3_raw0", "w1_lo"), load_rows(w3[PASS:, :], "w3_raw1", "w1_hi")]
+        w1_second_bf = held([P, PACK * PASS], BF16, "w1_second_bf", "rounded_w")
+        deal(on_scalar, w1_second_bf, w1_second[:, 0], 0, 0, P // 2)
+        deal(on_gpsimd, w1_second_bf, w1_second[:, 1], P // 2, P // 2, P)
 
-        y_scales = keep.tile([P, S], U8, name="y_scales", align_bytes=64)
-        y_codes = keep.tile([P, S], I32, name="y_codes", align_bytes=64)
+        y_scales = held([P, S], U8, "y_scales")
+        y_codes = held([P, S], I32, "y_codes")
         y_rows = out_0.rearrange("(p t) j -> p t j", t=PACK)
         y_words = out_1[0].rearrange("p m t -> p (m t)").bitcast(I32)
-        h, rounded = {}, {}
-        hq = {}
-        xs, ys, alives = {}, {}, {}
+        xs, alives, h, hq, ys, rounded = {}, {}, {}, {}, {}, {}
 
         def exposure(j0, width, s):
             x = ahead.tile([P, WIDE, PACK], F32, name="x")
@@ -183,15 +191,14 @@ def tile_list_survival_treatment_scores_kernel(
                 v_codes = vq[half][:, lo : lo + UNIT].bitcast(FP8X4)
                 v_scales = planes[:, H + j0 + u0 : H + j0 + u0 + UNIT]
                 unit = s * UNITS + (j0 + u0) // UNIT
-                a_ring, b_ring = ([0, 1, 5, 6], [2, 3, 4]) if s == 0 else ([0, 1], [2, 3, 4])
-                pa = bank(a_ring[unit % len(a_ring)], [P, PACK, UNIT])
-                pb = bank(b_ring[unit % len(b_ring)], [P, PACK, UNIT])
+                a_banks = A_BANKS if unit < A_LATE_FROM else A_BANKS_LATE
+                pa = bank(a_banks[unit % len(a_banks)], [P, PACK, UNIT])
+                pb = bank(B_BANKS[unit % len(B_BANKS)], [P, PACK, UNIT])
                 for t in range(PACK):
-                    c0 = s * PASS + t * P
                     nc.tensor.matmul_mx(
                         out=pb[:, t, :],
-                        lhsT=w2q[:, 2 * c0 : 2 * (c0 + P)].bitcast(FP4X4),
-                        lhsT_scale=planes[:, c0 : c0 + P],
+                        lhsT=w2q[s][:, 2 * t * P : 2 * (t + 1) * P].bitcast(FP4X4),
+                        lhsT_scale=planes[:, s * PASS + t * P : s * PASS + (t + 1) * P],
                         rhs=v_codes,
                         rhs_scale=v_scales,
                         start=True,
@@ -209,7 +216,7 @@ def tile_list_survival_treatment_scores_kernel(
                         stop=True,
                     )
                 if unit in (W1_AFTER, W3_AFTER - 1, W3_AFTER):
-                    hazard = keep.tile([P, UNIT, PACK], F32, name="hazard", tag=f"after{unit}", align_bytes=64)
+                    hazard = held([P, UNIT, PACK], F32, "hazard", f"after{unit}")
                 else:
                     hazard = ahead.tile([P, UNIT, PACK], F32, name="hazard")
                 nc.scalar.activation(hazard[:], pa[:].rearrange("p t n -> p n t"), EXP)
@@ -226,25 +233,24 @@ def tile_list_survival_treatment_scores_kernel(
         def survive(j0, width, s):
             alive = work.tile([P, WIDE, PACK], F32, name="alive")
             nc.scalar.activation(alive[:, :width, :], xs[j0, s][:, :width, :], EXP, scale=-1.0)
-            alives[j0, s] = alive
+            for u0 in range(0, width, UNIT):
+                alives[j0 + u0, s] = alive[:, u0:width, :]
 
-        def weigh(engine, factors, tag, j0, width, s):
-            step0 = j0 if (j0, s) in alives else j0 - UNIT
+        def weigh(engine, factors, j0, width, s, tag=None):
             if s == 0:
-                h[j0] = keep.tile([P, PASSES * width * PACK], BF16, name=f"h{j0}", tag=tag, align_bytes=64)
+                h[j0] = held([P, PASSES, width, PACK], BF16, f"h{j0}", tag)
             engine.tensor_tensor(
-                h[j0][:, s * width * PACK : (s + 1) * width * PACK].rearrange("p (n t) -> p n t", t=PACK),
-                alives[step0, s][:, j0 - step0 : j0 - step0 + width, :],
+                h[j0][:, s],
+                alives[j0, s][:, :width, :],
                 factors[:, s * PACK : (s + 1) * PACK].unsqueeze(1).to_broadcast([P, width, PACK]),
                 ALU.mult,
             )
 
-        def scores(j0, width):
+        def scores(j0, width, y_banks):
             per_bank = PASS // width
-            patients = slice(j0, j0 + width)
             y = keep.tile([P, PACK, width], F32, name=f"y{j0}")
             for t0 in range(0, PACK, per_bank):
-                py = bank(5 + t0 // per_bank if width == WIDE else j0 // UNIT % 2, [P, per_bank, width])
+                py = bank(y_banks[t0 // per_bank], [P, per_bank, width])
                 for t in range(t0, t0 + per_bank):
                     cols = slice(t * P, (t + 1) * P)
                     for s in range(PASSES):
@@ -258,65 +264,58 @@ def tile_list_survival_treatment_scores_kernel(
                             stop=(s == PASSES - 1),
                         )
                 nc.scalar.copy(y[:, t0 : t0 + per_bank, :], py[:])
-            nc.sync.dma_start(y_rows[:, :, patients], y[:])
+            nc.sync.dma_start(y_rows[:, :, j0 : j0 + width], y[:])
             ys[j0] = y
 
-        def round_scores(copy, piece, tag, j0, width):
-            rounded[j0] = keep.tile([P, width * PACK], BF16, name=f"rounded{j0}", tag=tag, align_bytes=64)
-            for lo in range(0, width, piece):
-                copy(
-                    rounded[j0][:, lo * PACK : (lo + piece) * PACK].rearrange("p (n t) -> p n t", t=PACK),
-                    ys[j0][:, :, lo : lo + piece].rearrange("p t n -> p n t"),
+        g_bank = bank(G_BANK, [P, P])
+        nc.tensor.transpose(g_bank[:], g_rows[:], identity[:])
+
+        exposure(0, WIDE, 0)
+        w2q.append(deal_w2(w2_second, "w2q1", "w1_second"))
+        w1q.append(quantise("w1_second", w1_second_bf, PASS, scales_tag=f"after{W1_AFTER}"))
+        w3_bf = [held([P, PACK * PASS], BF16, "w3_bf0", "rounded_w"), held([P, PACK * PASS], BF16, "w3_bf1")]
+        for s in range(PASSES):
+            deal(on_gpsimd, w3_bf[s], w3_raw[s][:], 0, 0, P)
+        for j0 in range(WIDE, S, WIDE):
+            exposure(j0, WIDE, 0)
+            survive(j0 - WIDE, WIDE, 0)
+            if j0 - WIDE < ON_VECTOR * WIDE:
+                weigh(nc.vector, g_bank, j0 - WIDE, WIDE, 0)
+
+        exposure(*GROUPS[0], 1)
+        w3q = [
+            quantise("w3_0", w3_bf[0], PASS, codes_tag="w1_hi", scales_tag=f"after{W3_AFTER}"),
+            quantise("w3_1", w3_bf[1], PASS, scales_tag=f"after{W3_AFTER - 1}"),
+        ]
+        weigh(nc.gpsimd, g_columns, *GROUPS[ON_VECTOR], 0, "rounded_w")
+        for c, (j0, width) in enumerate(GROUPS):
+            if c + 1 < len(GROUPS):
+                exposure(*GROUPS[c + 1], 1)
+            survive(j0, width, 1)
+            weigh(nc.vector, g_bank, j0, width, 1)
+            if c == 0:
+                survive(S - WIDE, WIDE, 0)
+            hq[j0] = quantise(f"h{j0}", h[j0][:].rearrange("p s n t -> p (s n t)"), PASSES * width)
+            if ON_VECTOR + 1 + c < len(GROUPS):
+                weigh(nc.gpsimd, g_columns, *GROUPS[ON_VECTOR + 1 + c], 0, f"h{j0}")
+
+        for (j0, width), y_banks in zip(GROUPS, Y_BANKS):
+            scores(j0, width, y_banks)
+
+        for c in range(len(GROUPS) + 1):
+            if c < len(GROUPS):
+                j0, width = GROUPS[c]
+                rounded[j0] = held([P, width, PACK], BF16, f"rounded{j0}")
+                nc.vector.tensor_copy(rounded[j0][:], ys[j0][:].rearrange("p t n -> p n t"))
+            if c > 0:
+                j0, width = GROUPS[c - 1]
+                nc.vector.quantize_mx(
+                    out=y_codes[:, j0 : j0 + width].bitcast(FP8X4),
+                    scales=y_scales[:, j0 : j0 + width],
+                    in_=rounded[j0][:].rearrange("p n t -> p (n t)"),
                 )
-
-        def quantise_columns(values, codes, scales, j0, width):
-            cols = slice(j0, j0 + width)
-            nc.vector.quantize_mx(out=codes[:, cols].bitcast(FP8X4), scales=scales[:, cols], in_=values[:])
-
-        first = len(STEPS) - len(GROUPS)
-        for i in range(len(STEPS) + 2):
-            if i < len(STEPS) - 1:
-                exposure(*STEPS[i])
-            if i == len(STEPS) - 1 - LEAD:
-                exposure(*STEPS[-1])
-            if i == W1_AFTER // 2:
-                w1q.append(quantise("w1_second", w1_second_bf, PASS, 1, "w1_second_codes", f"after{W1_AFTER}"))
-                for s in range(PASSES):
-                    w3_bf.append(keep.tile([P, PACK * PASS], BF16, name=f"w3_bf{s}", tag=f"rounded_w{s}", align_bytes=64))
-                    deal(w3_bf[s][:], [(on_gpsimd, w3_raw[s], 0, 0, P)])
-            if i == W3_AFTER // 2:
-                w3q.append(quantise("w3_0", w3_bf[0], PASS, 1, "early", f"after{W3_AFTER}"))
-                w3q.append(quantise("w3_1", w3_bf[1], PASS, 1, "w3_1_codes", f"after{W3_AFTER - 1}"))
-            if i == 0:
-                g_bank = bank(7, [P, P])
-                nc.tensor.transpose(g_bank[:], g_rows[:], identity[:])
-            if 0 <= i - 1 < len(STEPS):
-                j0, width, s = STEPS[i - 1]
-                survive(j0, width, s)
-                if i != first:
-                    weigh(nc.vector, g_bank, f"h{j0}", j0, width, s)
-                else:
-                    weigh(nc.gpsimd, g_columns, "rounded_w0", *GROUPS[-2], 0)
-                if s == 1:
-                    hq[j0] = quantise(f"h{j0}", h[j0], PASSES * width, 1, f"h{j0}_codes", f"h{j0}_scales")
-                if i - 1 == first:
-                    weigh(nc.gpsimd, g_columns, f"h{j0}", *GROUPS[-1], 0)
-                if i - 1 == first + 1:
-                    round_scores(on_gpsimd, WIDE, f"h{j0}", *GROUPS[0])
-            for c, group in enumerate(GROUPS):
-                if i == first + c + SCORE_LAGS[c] and group[0] not in ys:
-                    scores(*group)
-        round_scores(on_vector, WIDE, "rounded1", *GROUPS[1])
-        quantise_columns(rounded[0], y_codes, y_scales, *GROUPS[0])
-        round_scores(on_scalar, UNIT, "rounded2", *GROUPS[2])
-        quantise_columns(rounded[WIDE], y_codes, y_scales, *GROUPS[1])
-        round_scores(on_vector, UNIT, "rounded3", *GROUPS[3])
-        quantise_columns(rounded[2 * WIDE], y_codes, y_scales, *GROUPS[2])
-        round_scores(on_vector, UNIT, "rounded4", *GROUPS[4])
-        for j0, width in GROUPS[3:]:
-            quantise_columns(rounded[j0], y_codes, y_scales, j0, width)
-        for lo, hi in zip(CODE_STORES, CODE_STORES[1:]):
-            nc.sync.dma_start(y_words[:, lo:hi], y_codes[:, lo:hi])
+        for j0 in range(0, S, HALF):
+            nc.sync.dma_start(y_words[:, j0 : j0 + HALF], y_codes[:, j0 : j0 + HALF])
         for q, queue in enumerate([nc.sync, nc.scalar, nc.sync, nc.scalar]):
             queue.dma_start(
                 out_2[0, 4 * q : 4 * q + 4, :].bitcast(I32), y_scales[32 * q : 32 * q + 4, :].bitcast(I32)

@@ -29,8 +29,9 @@ HALF = S // 2
 WIDE = 2 * UNIT
 GROUPS = [(0, WIDE), (WIDE, WIDE), (2 * WIDE, WIDE), (3 * WIDE, UNIT), (3 * WIDE + UNIT, UNIT)]
 ON_VECTOR = 2
+ROUND_ON_SCALAR = 3
 SPLIT = 108
-W1_AFTER = 1
+W1_AFTER = 2
 W3_AFTER = UNITS + 1
 FINITE = 3.0e38
 
@@ -65,7 +66,7 @@ def tile_list_survival_treatment_scores_kernel(
         offsets = lists.tile([P, S // 16], U16, name="offsets")
         nc.sync.dma_start(offsets[:], offs)
 
-        tabs = held([P, T], U8, "tabs", "w1_second")
+        tabs = held([P, T], U8, "tabs")
         nc.sync.dma_start(tabs[ROW0:, :].bitcast(I32), tab_scales[0].bitcast(I32))
         nc.vector.memset(tabs[:ROW0, :].bitcast(I32), 0)
         w2s_raw = held([P, H], U8, "w2s_raw")
@@ -84,19 +85,6 @@ def tile_list_survival_treatment_scores_kernel(
         make_identity(nc, identity[:])
         g_turned = bank(G_TURN_BANK, [P, P])
         nc.tensor.transpose(g_turned[:], g_columns[:], identity[:])
-
-        def load_w2(s, tag):
-            raw = held([P, 2 * PASS], U8, f"w2_raw{s}", tag)
-            nc.sync.dma_start(raw[:].bitcast(I32), w2_words[0][:, 2 * s * PASS : 2 * (s + 1) * PASS].bitcast(I32))
-            return raw
-
-        def deal_w2(raw, name, tag):
-            words = held([P, 2 * PASS], U8, name, tag)
-            nc.vector.tensor_copy(
-                words[:].bitcast(U16).rearrange("p (t m) -> p t m", t=PACK),
-                raw[:].bitcast(U16).rearrange("p (m t) -> p t m", t=PACK),
-            )
-            return words
 
         def by_partition(rows):
             return rows.rearrange("(p j) c -> p j c", j=PACK)
@@ -129,17 +117,19 @@ def tile_list_survival_treatment_scores_kernel(
             nc.vector.tensor_copy(picked[:], tabs[:].indirect(offsets[:, cols]))
             return picked
 
-        def to_plane_rows(cols, source):
+        def to_plane_rows(queue, cols, source):
             for q in range(4):
-                nc.sync.dma_start(
+                queue.dma_start(
                     planes[32 * q : 32 * q + 4, cols].bitcast(I32),
                     source[ROW0 + 4 * q : ROW0 + 4 * q + 4, :].bitcast(I32),
                 )
 
-        w2_first = load_w2(0, "w1_hi")
+        w2_raw = held([P, 2 * H], U8, "w2_raw", "w1_second")
+        nc.sync.dma_start(w2_raw[:].bitcast(I32), w2_words[0].bitcast(I32))
         tabw = held([P, T], I32, "tabw")
         nc.sync.dma_start(tabw[:], tab_words[0].rearrange("p t i -> p (t i)").bitcast(I32))
         w1_lo = load_rows(w1[:, 0 : PASS // 2], "w1_lo", "w1_lo")
+        w1_hi = load_rows(w1[:, PASS // 2 : PASS], "w1_hi", "w1_hi")
 
         staged = held([P, H + HALF], U8, "staged")
         picked = pick_scales(0)
@@ -148,16 +138,16 @@ def tile_list_survival_treatment_scores_kernel(
             w2s_raw[:].rearrange("p (s m t) -> p s t m", s=PASSES, t=PACK),
         )
         nc.vector.tensor_copy(staged[:, H:].bitcast(I32), picked[:].bitcast(I32))
-        to_plane_rows(slice(0, H + HALF), staged)
-        w2q = [deal_w2(w2_first, "w2q0", None)]
-        w1_hi = load_rows(w1[:, PASS // 2 : PASS], "w1_hi", "w1_hi")
-        picked = pick_scales(1)
-        w1_second = held([P, 2, PACK, PASS // 2], F32, "w1_second")
-        for half in range(2):
-            c0 = PASS + half * PASS // 2
-            nc.sync.dma_start(w1_second[:, half], by_partition(w1[:, c0 : c0 + PASS // 2]))
-        to_plane_rows(slice(H + HALF, H + S), picked)
-        w2_second = load_w2(1, "staged")
+        to_plane_rows(nc.scalar, slice(0, H + HALF), staged)
+        w2q = held([P, 2 * H], U8, "w2q")
+        nc.vector.tensor_copy(
+            w2q[:].bitcast(U16).rearrange("p (s t m) -> p s t m", s=PASSES, t=PACK),
+            w2_raw[:].bitcast(U16).rearrange("p (s m t) -> p s t m", s=PASSES, t=PACK),
+        )
+        w1_second = load_rows(w1[:, PASS:], "w1_second", "w1_second")
+        to_plane_rows(nc.sync, slice(H + HALF, H + S), pick_scales(1))
+        g_unit = held([P, UNIT, PACK], F32, "g_unit", "w2s_raw")
+        nc.vector.tensor_copy(g_unit[:], g_columns[:, :PACK].unsqueeze(1).to_broadcast([P, UNIT, PACK]))
 
         vq = []
         for half in range(2):
@@ -171,12 +161,11 @@ def tile_list_survival_treatment_scores_kernel(
         deal(on_vector, w1_first_bf, w1_hi[:], P // 2, P // 2, SPLIT)
         deal(on_scalar, w1_first_bf, w1_hi[:], P // 2, SPLIT, P)
         w1q = [quantise("w1_first", w1_first_bf, PASS, calls=2)]
-        g_rows = held([P, P], F32, "g_rows")
+        g_rows = held([P, P], F32, "g_rows", "w1_first_bf")
         nc.vector.tensor_copy(g_rows[:], g_turned[:])
         w3_raw = [load_rows(w3[0:PASS, :], "w3_raw0", "w1_lo"), load_rows(w3[PASS:, :], "w3_raw1", "w1_hi")]
         w1_second_bf = held([P, PACK * PASS], BF16, "w1_second_bf", "rounded_w")
-        deal(on_scalar, w1_second_bf, w1_second[:, 0], 0, 0, P // 2)
-        deal(on_gpsimd, w1_second_bf, w1_second[:, 1], P // 2, P // 2, P)
+        deal(on_gpsimd, w1_second_bf, w1_second[:], 0, 0, P)
 
         y_scales = held([P, S], U8, "y_scales")
         y_codes = held([P, S], I32, "y_codes")
@@ -195,10 +184,11 @@ def tile_list_survival_treatment_scores_kernel(
                 pa = bank(a_banks[unit % len(a_banks)], [P, PACK, UNIT])
                 pb = bank(B_BANKS[unit % len(B_BANKS)], [P, PACK, UNIT])
                 for t in range(PACK):
+                    c0 = s * PASS + t * P
                     nc.tensor.matmul_mx(
                         out=pb[:, t, :],
-                        lhsT=w2q[s][:, 2 * t * P : 2 * (t + 1) * P].bitcast(FP4X4),
-                        lhsT_scale=planes[:, s * PASS + t * P : s * PASS + (t + 1) * P],
+                        lhsT=w2q[:, 2 * c0 : 2 * (c0 + P)].bitcast(FP4X4),
+                        lhsT_scale=planes[:, c0 : c0 + P],
                         rhs=v_codes,
                         rhs_scale=v_scales,
                         start=True,
@@ -236,13 +226,19 @@ def tile_list_survival_treatment_scores_kernel(
             for u0 in range(0, width, UNIT):
                 alives[j0 + u0, s] = alive[:, u0:width, :]
 
-        def weigh(engine, factors, j0, width, s, tag=None):
+        def weigh(j0, width, s):
             if s == 0:
-                h[j0] = held([P, PASSES, width, PACK], BF16, f"h{j0}", tag)
-            engine.tensor_tensor(
-                h[j0][:, s],
-                alives[j0, s][:, :width, :],
-                factors[:, s * PACK : (s + 1) * PACK].unsqueeze(1).to_broadcast([P, width, PACK]),
+                h[j0] = held([P, PASSES, width, PACK], BF16, f"h{j0}")
+            factors = g_bank[:, s * PACK : (s + 1) * PACK].unsqueeze(1).to_broadcast([P, width, PACK])
+            nc.vector.tensor_tensor(h[j0][:, s], alives[j0, s][:, :width, :], factors, ALU.mult)
+
+        def weigh_on_gpsimd(j0, width, tag):
+            h[j0] = held([P, PASSES, width, PACK], BF16, f"h{j0}", tag)
+            units = width // UNIT
+            nc.gpsimd.tensor_tensor(
+                h[j0][:, 0].rearrange("p (u n) t -> p u (n t)", u=units),
+                alives[j0, 0][:, :width, :].rearrange("p (u n) t -> p u (n t)", u=units),
+                g_unit[:].rearrange("p n t -> p (n t)").unsqueeze(1).to_broadcast([P, units, UNIT * PACK]),
                 ALU.mult,
             )
 
@@ -267,37 +263,36 @@ def tile_list_survival_treatment_scores_kernel(
             nc.sync.dma_start(y_rows[:, :, j0 : j0 + width], y[:])
             ys[j0] = y
 
+        exposure(0, WIDE, 0)
         g_bank = bank(G_BANK, [P, P])
         nc.tensor.transpose(g_bank[:], g_rows[:], identity[:])
-
-        exposure(0, WIDE, 0)
-        w2q.append(deal_w2(w2_second, "w2q1", "w1_second"))
-        w1q.append(quantise("w1_second", w1_second_bf, PASS, scales_tag=f"after{W1_AFTER}"))
-        w3_bf = [held([P, PACK * PASS], BF16, "w3_bf0", "rounded_w"), held([P, PACK * PASS], BF16, "w3_bf1")]
-        for s in range(PASSES):
-            deal(on_gpsimd, w3_bf[s], w3_raw[s][:], 0, 0, P)
         for j0 in range(WIDE, S, WIDE):
             exposure(j0, WIDE, 0)
+            if j0 == WIDE:
+                w1q.append(quantise("w1_second", w1_second_bf, PASS, scales_tag=f"after{W1_AFTER}"))
+                w3_bf = [held([P, PACK * PASS], BF16, "w3_bf0", "rounded_w"), held([P, PACK * PASS], BF16, "w3_bf1")]
+                for s in range(PASSES):
+                    deal(on_gpsimd, w3_bf[s], w3_raw[s][:], 0, 0, P)
             survive(j0 - WIDE, WIDE, 0)
             if j0 - WIDE < ON_VECTOR * WIDE:
-                weigh(nc.vector, g_bank, j0 - WIDE, WIDE, 0)
+                weigh(j0 - WIDE, WIDE, 0)
 
         exposure(*GROUPS[0], 1)
         w3q = [
             quantise("w3_0", w3_bf[0], PASS, codes_tag="w1_hi", scales_tag=f"after{W3_AFTER}"),
             quantise("w3_1", w3_bf[1], PASS, scales_tag=f"after{W3_AFTER - 1}"),
         ]
-        weigh(nc.gpsimd, g_columns, *GROUPS[ON_VECTOR], 0, "rounded_w")
+        weigh_on_gpsimd(*GROUPS[ON_VECTOR], "rounded_w")
         for c, (j0, width) in enumerate(GROUPS):
             if c + 1 < len(GROUPS):
                 exposure(*GROUPS[c + 1], 1)
             survive(j0, width, 1)
-            weigh(nc.vector, g_bank, j0, width, 1)
+            weigh(j0, width, 1)
             if c == 0:
                 survive(S - WIDE, WIDE, 0)
             hq[j0] = quantise(f"h{j0}", h[j0][:].rearrange("p s n t -> p (s n t)"), PASSES * width)
             if ON_VECTOR + 1 + c < len(GROUPS):
-                weigh(nc.gpsimd, g_columns, *GROUPS[ON_VECTOR + 1 + c], 0, f"h{j0}")
+                weigh_on_gpsimd(*GROUPS[ON_VECTOR + 1 + c], f"h{j0}")
 
         for (j0, width), y_banks in zip(GROUPS, Y_BANKS):
             scores(j0, width, y_banks)
@@ -306,7 +301,8 @@ def tile_list_survival_treatment_scores_kernel(
             if c < len(GROUPS):
                 j0, width = GROUPS[c]
                 rounded[j0] = held([P, width, PACK], BF16, f"rounded{j0}")
-                nc.vector.tensor_copy(rounded[j0][:], ys[j0][:].rearrange("p t n -> p n t"))
+                copy = on_scalar if c == ROUND_ON_SCALAR else on_vector
+                copy(rounded[j0][:], ys[j0][:].rearrange("p t n -> p n t"))
             if c > 0:
                 j0, width = GROUPS[c - 1]
                 nc.vector.quantize_mx(

@@ -30,9 +30,12 @@ WIDE = 2 * UNIT
 GROUPS = [(0, WIDE), (WIDE, WIDE), (2 * WIDE, WIDE), (3 * WIDE, UNIT), (3 * WIDE + UNIT, UNIT)]
 ON_VECTOR = 2
 ROUND_ON_SCALAR = 3
-SPLIT = 108
+PIECE = 96
+SPLITS = (40, 116)
+SECOND = 48
 W1_AFTER = 2
 W3_AFTER = UNITS + 1
+B_AHEAD = 3
 FINITE = 3.0e38
 
 A_BANKS, A_BANKS_LATE, A_LATE_FROM = (0, 1, 5, 6), (0, 1), UNITS + 4
@@ -72,8 +75,8 @@ def tile_list_survival_treatment_scores_kernel(
         w2s_raw = held([P, H], U8, "w2s_raw")
         nc.sync.dma_start(w2s_raw[ROW0:, :].bitcast(I32), w2_scales[0].bitcast(I32))
         nc.vector.memset(w2s_raw[:ROW0, :].bitcast(I32), 0)
-        planes = held([P, H + S], U8, "planes")
-        nc.vector.memset(planes[:].bitcast(I32), 0)
+        planes = held([P, 2, PASS + HALF], U8, "planes")
+        nc.vector.memset(planes[:].rearrange("p i c -> p (i c)").bitcast(I32), 0)
 
         g_columns = keep.tile([P, P], F32, name="g_columns")
         nc.scalar.dma_start(
@@ -111,43 +114,66 @@ def tile_list_survival_treatment_scores_kernel(
                 )
             return codes, scales
 
-        def pick_scales(half):
+        def place_scales(part, queue):
             picked = held([P, HALF], U8, "picked")
-            cols = slice(half * HALF // 16, (half + 1) * HALF // 16)
+            cols = slice(part * HALF // 16, (part + 1) * HALF // 16)
             nc.vector.tensor_copy(picked[:], tabs[:].indirect(offsets[:, cols]))
-            return picked
-
-        def to_plane_rows(queue, cols, source):
+            staged = held([P, PASS + HALF], U8, f"staged{part}")
+            nc.vector.tensor_copy(
+                staged[:, :PASS].rearrange("p (t m) -> p t m", t=PACK),
+                w2s_raw[:, part * PASS : (part + 1) * PASS].rearrange("p (m t) -> p t m", t=PACK),
+            )
+            nc.vector.tensor_copy(staged[:, PASS:].bitcast(I32), picked[:].bitcast(I32))
             for q in range(4):
                 queue.dma_start(
-                    planes[32 * q : 32 * q + 4, cols].bitcast(I32),
-                    source[ROW0 + 4 * q : ROW0 + 4 * q + 4, :].bitcast(I32),
+                    planes[32 * q : 32 * q + 4, part, :].bitcast(I32),
+                    staged[ROW0 + 4 * q : ROW0 + 4 * q + 4, :].bitcast(I32),
                 )
 
-        w2_raw = held([P, 2 * H], U8, "w2_raw", "w1_second")
-        nc.sync.dma_start(w2_raw[:].bitcast(I32), w2_words[0].bitcast(I32))
+        def load_w2(s, tag):
+            raw = held([P, 2 * PASS], U8, f"w2_raw{s}", tag)
+            nc.sync.dma_start(raw[:].bitcast(I32), w2_words[0, :, 2 * s * PASS : 2 * (s + 1) * PASS].bitcast(I32))
+            return raw
+
+        def deal_w2(s, raw, tag=None):
+            words = held([P, 2 * PASS], U8, f"w2q{s}", tag)
+            nc.vector.tensor_copy(
+                words[:].bitcast(U16).rearrange("p (t m) -> p t m", t=PACK),
+                raw[:].bitcast(U16).rearrange("p (m t) -> p t m", t=PACK),
+            )
+            return words
+
+        w2_first = load_w2(0, "w1_second")
         tabw = held([P, T], I32, "tabw")
         nc.sync.dma_start(tabw[:], tab_words[0].rearrange("p t i -> p (t i)").bitcast(I32))
-        w1_lo = load_rows(w1[:, 0 : PASS // 2], "w1_lo", "w1_lo")
-        w1_hi = load_rows(w1[:, PASS // 2 : PASS], "w1_hi", "w1_hi")
+        w1_lo = load_rows(w1[:, 0 : PACK * PIECE], "w1_lo", "w1_lo")
+        w1_hi = load_rows(w1[:, PACK * PIECE : PASS], "w1_hi", "w1_hi")
+        w2_second = load_w2(1, "w2_second")
 
-        staged = held([P, H + HALF], U8, "staged")
-        picked = pick_scales(0)
+        place_scales(0, nc.scalar)
+        w2q = [deal_w2(0, w2_first)]
+        w1_rest = held([P, PACK * PASS], F32, "w1_second")
+        cut = PACK * SECOND
+        w1_second = [
+            w1_rest[:, : PACK * cut].rearrange("p (j c) -> p j c", j=PACK),
+            w1_rest[:, PACK * cut :].rearrange("p (j c) -> p j c", j=PACK),
+        ]
+        nc.sync.dma_start(w1_second[0], by_partition(w1[:, PASS : PASS + cut]))
+        nc.sync.dma_start(w1_second[1], by_partition(w1[:, PASS + cut :]))
+        place_scales(1, nc.sync)
+        g_unit = held([P, PASSES, UNIT, PACK], F32, "g_unit", "w2s_raw")
         nc.vector.tensor_copy(
-            staged[:, :H].rearrange("p (s t m) -> p s t m", s=PASSES, t=PACK),
-            w2s_raw[:].rearrange("p (s m t) -> p s t m", s=PASSES, t=PACK),
+            g_unit[:],
+            g_columns[:, : PASSES * PACK]
+            .rearrange("p (s t) -> p s t", t=PACK)
+            .unsqueeze(2)
+            .to_broadcast([P, PASSES, UNIT, PACK]),
         )
-        nc.vector.tensor_copy(staged[:, H:].bitcast(I32), picked[:].bitcast(I32))
-        to_plane_rows(nc.scalar, slice(0, H + HALF), staged)
-        w2q = held([P, 2 * H], U8, "w2q")
-        nc.vector.tensor_copy(
-            w2q[:].bitcast(U16).rearrange("p (s t m) -> p s t m", s=PASSES, t=PACK),
-            w2_raw[:].bitcast(U16).rearrange("p (s m t) -> p s t m", s=PASSES, t=PACK),
-        )
-        w1_second = load_rows(w1[:, PASS:], "w1_second", "w1_second")
-        to_plane_rows(nc.sync, slice(H + HALF, H + S), pick_scales(1))
-        g_unit = held([P, UNIT, PACK], F32, "g_unit", "w2s_raw")
-        nc.vector.tensor_copy(g_unit[:], g_columns[:, :PACK].unsqueeze(1).to_broadcast([P, UNIT, PACK]))
+
+        g_rows = held([P, P], F32, "g_rows", "picked")
+        nc.vector.tensor_copy(g_rows[:], g_turned[:])
+        g_bank = bank(G_BANK, [P, P])
+        nc.tensor.transpose(g_bank[:], g_rows[:], identity[:])
 
         vq = []
         for half in range(2):
@@ -157,15 +183,28 @@ def tile_list_survival_treatment_scores_kernel(
             vq.append(words)
 
         w1_first_bf = held([P, PACK * PASS], BF16, "w1_first_bf")
-        deal(on_scalar, w1_first_bf, w1_lo[:], 0, 0, P // 2)
-        deal(on_vector, w1_first_bf, w1_hi[:], P // 2, P // 2, SPLIT)
-        deal(on_scalar, w1_first_bf, w1_hi[:], P // 2, SPLIT, P)
-        w1q = [quantise("w1_first", w1_first_bf, PASS, calls=2)]
-        g_rows = held([P, P], F32, "g_rows", "w1_first_bf")
-        nc.vector.tensor_copy(g_rows[:], g_turned[:])
+        w1_first = held([P, PASS], U32, "w1_first_codes"), held([P, PASS], U8, "w1_first_scales")
+
+        def quantise_half_slots(m0):
+            for c0 in range(m0, PASS, P):
+                nc.vector.quantize_mx(
+                    out=w1_first[0][:, c0 : c0 + P // 2].bitcast(FP8X4),
+                    scales=w1_first[1][:, c0 : c0 + P // 2],
+                    in_=w1_first_bf[:, PACK * c0 : PACK * (c0 + P // 2)],
+                )
+
+        deal(on_scalar, w1_first_bf, w1_lo[:], 0, 0, SPLITS[0])
+        deal(on_vector, w1_first_bf, w1_lo[:], 0, SPLITS[0], PIECE)
+        deal(on_vector, w1_first_bf, w1_hi[:], PIECE, PIECE, SPLITS[1])
+        deal(on_scalar, w1_first_bf, w1_hi[:], PIECE, SPLITS[1], P)
+        quantise_half_slots(0)
+        quantise_half_slots(P // 2)
+        w1q = [w1_first]
+        w2q.append(deal_w2(1, w2_second, "w1_first_bf"))
         w3_raw = [load_rows(w3[0:PASS, :], "w3_raw0", "w1_lo"), load_rows(w3[PASS:, :], "w3_raw1", "w1_hi")]
         w1_second_bf = held([P, PACK * PASS], BF16, "w1_second_bf", "rounded_w")
-        deal(on_gpsimd, w1_second_bf, w1_second[:], 0, 0, P)
+        deal(on_vector, w1_second_bf, w1_second[0], 0, 0, SECOND)
+        deal(on_gpsimd, w1_second_bf, w1_second[1], SECOND, SECOND, P)
 
         y_scales = held([P, S], U8, "y_scales")
         y_codes = held([P, S], I32, "y_codes")
@@ -173,38 +212,35 @@ def tile_list_survival_treatment_scores_kernel(
         y_words = out_1[0].rearrange("p m t -> p (m t)").bitcast(I32)
         xs, alives, h, hq, ys, rounded = {}, {}, {}, {}, {}, {}
 
+        def product(out, codes, scales, unit):
+            half, lo = divmod(unit % UNITS * UNIT, HALF)
+            for t in range(PACK):
+                nc.tensor.matmul_mx(
+                    out=out[:, t, :],
+                    lhsT=codes(t * P),
+                    lhsT_scale=scales[:, t * P : (t + 1) * P],
+                    rhs=vq[half][:, lo : lo + UNIT].bitcast(FP8X4),
+                    rhs_scale=planes[:, half, PASS + lo : PASS + lo + UNIT],
+                    start=True,
+                    stop=True,
+                )
+
+        def follow_up(unit):
+            s = unit // UNITS
+            pb = bank(B_BANKS[unit % len(B_BANKS)], [P, PACK, UNIT])
+            product(pb, lambda c0: w2q[s][:, 2 * c0 : 2 * (c0 + P)].bitcast(FP4X4), planes[:, s, :PASS], unit)
+            return pb
+
+        b_ahead = [follow_up(unit) for unit in range(B_AHEAD)]
+
         def exposure(j0, width, s):
             x = ahead.tile([P, WIDE, PACK], F32, name="x")
             for u0 in range(0, width, UNIT):
-                half, lo = divmod(j0 + u0, HALF)
-                v_codes = vq[half][:, lo : lo + UNIT].bitcast(FP8X4)
-                v_scales = planes[:, H + j0 + u0 : H + j0 + u0 + UNIT]
                 unit = s * UNITS + (j0 + u0) // UNIT
                 a_banks = A_BANKS if unit < A_LATE_FROM else A_BANKS_LATE
                 pa = bank(a_banks[unit % len(a_banks)], [P, PACK, UNIT])
-                pb = bank(B_BANKS[unit % len(B_BANKS)], [P, PACK, UNIT])
-                for t in range(PACK):
-                    c0 = s * PASS + t * P
-                    nc.tensor.matmul_mx(
-                        out=pb[:, t, :],
-                        lhsT=w2q[:, 2 * c0 : 2 * (c0 + P)].bitcast(FP4X4),
-                        lhsT_scale=planes[:, c0 : c0 + P],
-                        rhs=v_codes,
-                        rhs_scale=v_scales,
-                        start=True,
-                        stop=True,
-                    )
-                for t in range(PACK):
-                    cols = slice(t * P, (t + 1) * P)
-                    nc.tensor.matmul_mx(
-                        out=pa[:, t, :],
-                        lhsT=w1q[s][0][:, cols].bitcast(FP8X4),
-                        lhsT_scale=w1q[s][1][:, cols],
-                        rhs=v_codes,
-                        rhs_scale=v_scales,
-                        start=True,
-                        stop=True,
-                    )
+                product(pa, lambda c0: w1q[s][0][:, c0 : c0 + P].bitcast(FP8X4), w1q[s][1], unit)
+                pb = b_ahead[unit] if unit < B_AHEAD else follow_up(unit)
                 if unit in (W1_AFTER, W3_AFTER - 1, W3_AFTER):
                     hazard = held([P, UNIT, PACK], F32, "hazard", f"after{unit}")
                 else:
@@ -238,7 +274,7 @@ def tile_list_survival_treatment_scores_kernel(
             nc.gpsimd.tensor_tensor(
                 h[j0][:, 0].rearrange("p (u n) t -> p u (n t)", u=units),
                 alives[j0, 0][:, :width, :].rearrange("p (u n) t -> p u (n t)", u=units),
-                g_unit[:].rearrange("p n t -> p (n t)").unsqueeze(1).to_broadcast([P, units, UNIT * PACK]),
+                g_unit[:, 0].rearrange("p n t -> p (n t)").unsqueeze(1).to_broadcast([P, units, UNIT * PACK]),
                 ALU.mult,
             )
 
@@ -264,8 +300,6 @@ def tile_list_survival_treatment_scores_kernel(
             ys[j0] = y
 
         exposure(0, WIDE, 0)
-        g_bank = bank(G_BANK, [P, P])
-        nc.tensor.transpose(g_bank[:], g_rows[:], identity[:])
         for j0 in range(WIDE, S, WIDE):
             exposure(j0, WIDE, 0)
             if j0 == WIDE:

@@ -31,16 +31,16 @@ GROUPS = [(0, WIDE), (WIDE, WIDE), (2 * WIDE, WIDE), (3 * WIDE, UNIT), (3 * WIDE
 ON_VECTOR = 2
 ROUND_ON_SCALAR = 3
 PIECE = 96
-SPLITS = (40, 116)
-SECOND = 48
+SPLITS = (32, 116)
 W1_AFTER = 2
-W3_AFTER = UNITS + 1
-B_AHEAD = 3
+W3_AFTER = UNITS
+B_AHEAD = 1
+CODE_STORES = [(0, 512), (512, 768), (768, 1024)]
 FINITE = 3.0e38
 
 A_BANKS, A_BANKS_LATE, A_LATE_FROM = (0, 1, 5, 6), (0, 1), UNITS + 4
-B_BANKS = (2, 3, 4)
-Y_BANKS = ((5, 6), (5, 6), (0, 1), (2,), (3,))
+B_BANKS, B_BANKS_EARLY = (2, 3, 4), (2, 4)
+Y_BANKS = ((5, 6), (5, 6), (0, 1), (3,), (4,))
 G_BANK, G_TURN_BANK = 7, 4
 
 
@@ -53,6 +53,7 @@ def tile_list_survival_treatment_scores_kernel(
         keep = ctx.enter_context(tc.tile_pool(name="keep", bufs=1))
         work = ctx.enter_context(tc.tile_pool(name="work", bufs=4))
         ahead = ctx.enter_context(tc.tile_pool(name="ahead", bufs=6))
+        after_w1 = ctx.enter_context(tc.tile_pool(name="after_w1", bufs=1))
         banks = ctx.enter_context(tc.psum_pool(name="banks", bufs=1))
 
         def bank(number, shape):
@@ -78,7 +79,7 @@ def tile_list_survival_treatment_scores_kernel(
         planes = held([P, 2, PASS + HALF], U8, "planes")
         nc.vector.memset(planes[:].rearrange("p i c -> p (i c)").bitcast(I32), 0)
 
-        g_columns = keep.tile([P, P], F32, name="g_columns")
+        g_columns = held([P, P], F32, "g_columns")
         nc.scalar.dma_start(
             g_columns[:, : PASSES * PACK].rearrange("p (s t) -> p s t", t=PACK),
             g.rearrange("(s p t) -> p s t", t=PACK, p=P),
@@ -115,7 +116,7 @@ def tile_list_survival_treatment_scores_kernel(
             return codes, scales
 
         def place_scales(part, queue):
-            picked = held([P, HALF], U8, "picked")
+            picked = held([P, HALF], U8, f"picked{part}")
             cols = slice(part * HALF // 16, (part + 1) * HALF // 16)
             nc.vector.tensor_copy(picked[:], tabs[:].indirect(offsets[:, cols]))
             staged = held([P, PASS + HALF], U8, f"staged{part}")
@@ -124,11 +125,8 @@ def tile_list_survival_treatment_scores_kernel(
                 w2s_raw[:, part * PASS : (part + 1) * PASS].rearrange("p (m t) -> p t m", t=PACK),
             )
             nc.vector.tensor_copy(staged[:, PASS:].bitcast(I32), picked[:].bitcast(I32))
-            for q in range(4):
-                queue.dma_start(
-                    planes[32 * q : 32 * q + 4, part, :].bitcast(I32),
-                    staged[ROW0 + 4 * q : ROW0 + 4 * q + 4, :].bitcast(I32),
-                )
+            for r in range(4):
+                queue.dma_start(planes[r:P:32, part, :].bitcast(I32), staged[ROW0 + r : P : 4, :].bitcast(I32))
 
         def load_w2(s, tag):
             raw = held([P, 2 * PASS], U8, f"w2_raw{s}", tag)
@@ -143,74 +141,46 @@ def tile_list_survival_treatment_scores_kernel(
             )
             return words
 
-        w2_first = load_w2(0, "w1_second")
+        w2_first = load_w2(0, "w2_raw")
         tabw = held([P, T], I32, "tabw")
         nc.sync.dma_start(tabw[:], tab_words[0].rearrange("p t i -> p (t i)").bitcast(I32))
         w1_lo = load_rows(w1[:, 0 : PACK * PIECE], "w1_lo", "w1_lo")
         w1_hi = load_rows(w1[:, PACK * PIECE : PASS], "w1_hi", "w1_hi")
-        w2_second = load_w2(1, "w2_second")
 
         place_scales(0, nc.scalar)
         w2q = [deal_w2(0, w2_first)]
-        w1_rest = held([P, PACK * PASS], F32, "w1_second")
-        cut = PACK * SECOND
-        w1_second = [
-            w1_rest[:, : PACK * cut].rearrange("p (j c) -> p j c", j=PACK),
-            w1_rest[:, PACK * cut :].rearrange("p (j c) -> p j c", j=PACK),
-        ]
-        nc.sync.dma_start(w1_second[0], by_partition(w1[:, PASS : PASS + cut]))
-        nc.sync.dma_start(w1_second[1], by_partition(w1[:, PASS + cut :]))
+        w2_second = load_w2(1, "w2_raw")
+        g_unit = held([P, UNIT, PACK], F32, "g_unit", "picked0")
+        nc.vector.tensor_copy(g_unit[:], g_columns[:, :PACK].unsqueeze(1).to_broadcast([P, UNIT, PACK]))
+        w1_second = load_rows(w1[:, PASS:], "w1_second", "g_columns")
         place_scales(1, nc.sync)
-        g_unit = held([P, PASSES, UNIT, PACK], F32, "g_unit", "w2s_raw")
-        nc.vector.tensor_copy(
-            g_unit[:],
-            g_columns[:, : PASSES * PACK]
-            .rearrange("p (s t) -> p s t", t=PACK)
-            .unsqueeze(2)
-            .to_broadcast([P, PASSES, UNIT, PACK]),
-        )
 
-        g_rows = held([P, P], F32, "g_rows", "picked")
-        nc.vector.tensor_copy(g_rows[:], g_turned[:])
-        g_bank = bank(G_BANK, [P, P])
-        nc.tensor.transpose(g_bank[:], g_rows[:], identity[:])
-
-        vq = []
-        for half in range(2):
-            words = held([P, HALF], U32, f"vq{half}")
+        def pick_words(half, words):
             cols = slice(half * HALF // 16, (half + 1) * HALF // 16)
             nc.vector.tensor_copy(words[:], tabw[:].bitcast(U32).indirect(offsets[:, cols]))
-            vq.append(words)
+            return words
 
-        w1_first_bf = held([P, PACK * PASS], BF16, "w1_first_bf")
-        w1_first = held([P, PASS], U32, "w1_first_codes"), held([P, PASS], U8, "w1_first_scales")
-
-        def quantise_half_slots(m0):
-            for c0 in range(m0, PASS, P):
-                nc.vector.quantize_mx(
-                    out=w1_first[0][:, c0 : c0 + P // 2].bitcast(FP8X4),
-                    scales=w1_first[1][:, c0 : c0 + P // 2],
-                    in_=w1_first_bf[:, PACK * c0 : PACK * (c0 + P // 2)],
-                )
-
+        vq = [pick_words(0, held([P, HALF], U32, "vq0"))]
+        w1_first_bf = after_w1.tile([P, PACK * PASS], BF16, name="w1_first_bf", offset=0, align_bytes=64)
         deal(on_scalar, w1_first_bf, w1_lo[:], 0, 0, SPLITS[0])
         deal(on_vector, w1_first_bf, w1_lo[:], 0, SPLITS[0], PIECE)
         deal(on_vector, w1_first_bf, w1_hi[:], PIECE, PIECE, SPLITS[1])
         deal(on_scalar, w1_first_bf, w1_hi[:], PIECE, SPLITS[1], P)
-        quantise_half_slots(0)
-        quantise_half_slots(P // 2)
-        w1q = [w1_first]
-        w2q.append(deal_w2(1, w2_second, "w1_first_bf"))
+        w1q = [quantise("w1_first", w1_first_bf, PASS, calls=2)]
+        g_rows = after_w1.tile([P, P], F32, name="g_rows", offset=0, align_bytes=64)
+        nc.vector.tensor_copy(g_rows[:], g_turned[:])
+        vq.append(pick_words(1, after_w1.tile([P, HALF], U32, name="vq1", offset=4 * HALF, align_bytes=64)))
+        w2q.append(deal_w2(1, w2_second, "tabw"))
         w3_raw = [load_rows(w3[0:PASS, :], "w3_raw0", "w1_lo"), load_rows(w3[PASS:, :], "w3_raw1", "w1_hi")]
         w1_second_bf = held([P, PACK * PASS], BF16, "w1_second_bf", "rounded_w")
-        deal(on_vector, w1_second_bf, w1_second[0], 0, 0, SECOND)
-        deal(on_gpsimd, w1_second_bf, w1_second[1], SECOND, SECOND, P)
+        deal(on_gpsimd, w1_second_bf, w1_second[:], 0, 0, P)
 
+        y_all = keep.tile([P, PACK, S], F32, name="y_all")
         y_scales = held([P, S], U8, "y_scales")
         y_codes = held([P, S], I32, "y_codes")
         y_rows = out_0.rearrange("(p t) j -> p t j", t=PACK)
         y_words = out_1[0].rearrange("p m t -> p (m t)").bitcast(I32)
-        xs, alives, h, hq, ys, rounded = {}, {}, {}, {}, {}, {}
+        xs, alives, h, hq = {}, {}, {}, {}
 
         def product(out, codes, scales, unit):
             half, lo = divmod(unit % UNITS * UNIT, HALF)
@@ -227,7 +197,8 @@ def tile_list_survival_treatment_scores_kernel(
 
         def follow_up(unit):
             s = unit // UNITS
-            pb = bank(B_BANKS[unit % len(B_BANKS)], [P, PACK, UNIT])
+            b_banks = B_BANKS_EARLY if unit < UNITS // 2 else B_BANKS
+            pb = bank(b_banks[unit % len(b_banks)], [P, PACK, UNIT])
             product(pb, lambda c0: w2q[s][:, 2 * c0 : 2 * (c0 + P)].bitcast(FP4X4), planes[:, s, :PASS], unit)
             return pb
 
@@ -241,7 +212,7 @@ def tile_list_survival_treatment_scores_kernel(
                 pa = bank(a_banks[unit % len(a_banks)], [P, PACK, UNIT])
                 product(pa, lambda c0: w1q[s][0][:, c0 : c0 + P].bitcast(FP8X4), w1q[s][1], unit)
                 pb = b_ahead[unit] if unit < B_AHEAD else follow_up(unit)
-                if unit in (W1_AFTER, W3_AFTER - 1, W3_AFTER):
+                if unit in (W1_AFTER, W3_AFTER):
                     hazard = held([P, UNIT, PACK], F32, "hazard", f"after{unit}")
                 else:
                     hazard = ahead.tile([P, UNIT, PACK], F32, name="hazard")
@@ -274,13 +245,13 @@ def tile_list_survival_treatment_scores_kernel(
             nc.gpsimd.tensor_tensor(
                 h[j0][:, 0].rearrange("p (u n) t -> p u (n t)", u=units),
                 alives[j0, 0][:, :width, :].rearrange("p (u n) t -> p u (n t)", u=units),
-                g_unit[:, 0].rearrange("p n t -> p (n t)").unsqueeze(1).to_broadcast([P, units, UNIT * PACK]),
+                g_unit[:].rearrange("p n t -> p (n t)").unsqueeze(1).to_broadcast([P, units, UNIT * PACK]),
                 ALU.mult,
             )
 
         def scores(j0, width, y_banks):
             per_bank = PASS // width
-            y = keep.tile([P, PACK, width], F32, name=f"y{j0}")
+            y = y_all[:, :, j0 : j0 + width]
             for t0 in range(0, PACK, per_bank):
                 py = bank(y_banks[t0 // per_bank], [P, per_bank, width])
                 for t in range(t0, t0 + per_bank):
@@ -295,27 +266,27 @@ def tile_list_survival_treatment_scores_kernel(
                             start=(s == 0),
                             stop=(s == PASSES - 1),
                         )
-                nc.scalar.copy(y[:, t0 : t0 + per_bank, :], py[:])
-            nc.sync.dma_start(y_rows[:, :, j0 : j0 + width], y[:])
-            ys[j0] = y
+                slots = slice(t0, t0 + per_bank)
+                nc.scalar.copy(y[:, slots, :], py[:])
+                nc.sync.dma_start(y_rows[:, slots, j0 : j0 + width], y[:, slots, :])
 
         exposure(0, WIDE, 0)
+        g_bank = bank(G_BANK, [P, P])
+        nc.tensor.transpose(g_bank[:], g_rows[:], identity[:])
         for j0 in range(WIDE, S, WIDE):
             exposure(j0, WIDE, 0)
             if j0 == WIDE:
                 w1q.append(quantise("w1_second", w1_second_bf, PASS, scales_tag=f"after{W1_AFTER}"))
-                w3_bf = [held([P, PACK * PASS], BF16, "w3_bf0", "rounded_w"), held([P, PACK * PASS], BF16, "w3_bf1")]
+                w3_bf = held([P, PASSES * PACK * PASS], BF16, "w3_bf", "rounded_w")
                 for s in range(PASSES):
-                    deal(on_gpsimd, w3_bf[s], w3_raw[s][:], 0, 0, P)
+                    deal(on_gpsimd, w3_bf[:, s * PACK * PASS : (s + 1) * PACK * PASS], w3_raw[s][:], 0, 0, P)
             survive(j0 - WIDE, WIDE, 0)
             if j0 - WIDE < ON_VECTOR * WIDE:
                 weigh(j0 - WIDE, WIDE, 0)
 
         exposure(*GROUPS[0], 1)
-        w3q = [
-            quantise("w3_0", w3_bf[0], PASS, codes_tag="w1_hi", scales_tag=f"after{W3_AFTER}"),
-            quantise("w3_1", w3_bf[1], PASS, scales_tag=f"after{W3_AFTER - 1}"),
-        ]
+        w3_codes, w3_scales = quantise("w3", w3_bf, PASSES * PASS, scales_tag=f"after{W3_AFTER}")
+        w3q = [(w3_codes[:, s * PASS : (s + 1) * PASS], w3_scales[:, s * PASS : (s + 1) * PASS]) for s in range(PASSES)]
         weigh_on_gpsimd(*GROUPS[ON_VECTOR], "rounded_w")
         for c, (j0, width) in enumerate(GROUPS):
             if c + 1 < len(GROUPS):
@@ -331,21 +302,27 @@ def tile_list_survival_treatment_scores_kernel(
         for (j0, width), y_banks in zip(GROUPS, Y_BANKS):
             scores(j0, width, y_banks)
 
-        for c in range(len(GROUPS) + 1):
-            if c < len(GROUPS):
-                j0, width = GROUPS[c]
-                rounded[j0] = held([P, width, PACK], BF16, f"rounded{j0}")
-                copy = on_scalar if c == ROUND_ON_SCALAR else on_vector
-                copy(rounded[j0][:], ys[j0][:].rearrange("p t n -> p n t"))
-            if c > 0:
-                j0, width = GROUPS[c - 1]
-                nc.vector.quantize_mx(
-                    out=y_codes[:, j0 : j0 + width].bitcast(FP8X4),
-                    scales=y_scales[:, j0 : j0 + width],
-                    in_=rounded[j0][:].rearrange("p n t -> p (n t)"),
-                )
-        for j0 in range(0, S, HALF):
-            nc.sync.dma_start(y_words[:, j0 : j0 + HALF], y_codes[:, j0 : j0 + HALF])
+        rounded = held([P, S, PACK], BF16, "rounded")
+
+        def round_y(copy, j0, j1):
+            copy(rounded[:, j0:j1, :], y_all[:, :, j0:j1].rearrange("p t n -> p n t"))
+
+        def quantise_y(j0, j1):
+            nc.vector.quantize_mx(
+                out=y_codes[:, j0:j1].bitcast(FP8X4),
+                scales=y_scales[:, j0:j1],
+                in_=rounded[:, j0:j1, :].rearrange("p n t -> p (n t)"),
+            )
+
+        round_y(on_vector, 0, HALF)
+        round_y(on_vector, HALF, HALF + WIDE)
+        quantise_y(0, HALF)
+        round_y(on_scalar, HALF + WIDE, S - UNIT)
+        round_y(on_vector, S - UNIT, S)
+        quantise_y(HALF, HALF + WIDE)
+        quantise_y(HALF + WIDE, S)
+        for j0, j1 in CODE_STORES:
+            nc.sync.dma_start(y_words[:, j0:j1], y_codes[:, j0:j1])
         for q, queue in enumerate([nc.sync, nc.scalar, nc.sync, nc.scalar]):
             queue.dma_start(
                 out_2[0, 4 * q : 4 * q + 4, :].bitcast(I32), y_scales[32 * q : 32 * q + 4, :].bitcast(I32)

@@ -32,6 +32,7 @@ ON_VECTOR = 2
 ROUND_ON_SCALAR = 3
 PIECE = 96
 SPLITS = (32, 116)
+SECOND = 48
 W1_AFTER = 2
 W3_AFTER = UNITS
 B_AHEAD = 1
@@ -65,7 +66,7 @@ def tile_list_survival_treatment_scores_kernel(
         on_vector, on_scalar = nc.vector.tensor_copy, nc.scalar.copy
 
         def on_gpsimd(dst, src):
-            nc.gpsimd.tensor_scalar(dst, src, 1.0, 0.0, ALU.mult, ALU.add)
+            nc.gpsimd.tensor_scalar(dst, src, one[:], 0.0, ALU.mult, ALU.add)
 
         offsets = lists.tile([P, S // 16], U16, name="offsets")
         nc.sync.dma_start(offsets[:], offs)
@@ -152,7 +153,14 @@ def tile_list_survival_treatment_scores_kernel(
         w2_second = load_w2(1, "w2_raw")
         g_unit = held([P, UNIT, PACK], F32, "g_unit", "picked0")
         nc.vector.tensor_copy(g_unit[:], g_columns[:, :PACK].unsqueeze(1).to_broadcast([P, UNIT, PACK]))
-        w1_second = load_rows(w1[:, PASS:], "w1_second", "g_columns")
+        w1_rest = held([P, PACK * PASS], F32, "w1_rest", "g_columns")
+        cut = PACK * SECOND
+        w1_second = [
+            w1_rest[:, : PACK * cut].rearrange("p (j c) -> p j c", j=PACK),
+            w1_rest[:, PACK * cut :].rearrange("p (j c) -> p j c", j=PACK),
+        ]
+        nc.sync.dma_start(w1_second[0], by_partition(w1[:, PASS : PASS + cut]))
+        nc.sync.dma_start(w1_second[1], by_partition(w1[:, PASS + cut :]))
         place_scales(1, nc.sync)
 
         def pick_words(half, words):
@@ -173,7 +181,10 @@ def tile_list_survival_treatment_scores_kernel(
         w2q.append(deal_w2(1, w2_second, "tabw"))
         w3_raw = [load_rows(w3[0:PASS, :], "w3_raw0", "w1_lo"), load_rows(w3[PASS:, :], "w3_raw1", "w1_hi")]
         w1_second_bf = held([P, PACK * PASS], BF16, "w1_second_bf", "rounded_w")
-        deal(on_gpsimd, w1_second_bf, w1_second[:], 0, 0, P)
+        deal(on_scalar, w1_second_bf, w1_second[0], 0, 0, SECOND)
+        one = held([P, 1], F32, "one", "w2_raw")
+        nc.gpsimd.memset(one[:], 1.0)
+        deal(on_gpsimd, w1_second_bf, w1_second[1], SECOND, SECOND, P)
 
         y_all = keep.tile([P, PACK, S], F32, name="y_all")
         y_scales = held([P, S], U8, "y_scales")

@@ -32,15 +32,15 @@ ON_VECTOR = 2
 ROUND_ON_SCALAR = 3
 PIECE = 96
 SPLITS = (32, 116)
-SECOND = 48
+SECOND = 64
 W1_AFTER = 2
 W3_AFTER = UNITS
-B_AHEAD = 1
+B_AHEAD = 2
 CODE_STORES = [(0, 512), (512, 768), (768, 1024)]
 FINITE = 3.0e38
 
 A_BANKS, A_BANKS_LATE, A_LATE_FROM = (0, 1, 5, 6), (0, 1), UNITS + 4
-B_BANKS, B_BANKS_EARLY = (2, 3, 4), (2, 4)
+B_BANKS = (2, 3, 4)
 Y_BANKS = ((5, 6), (5, 6), (0, 1), (3,), (4,))
 G_BANK, G_TURN_BANK = 7, 4
 
@@ -150,16 +150,16 @@ def tile_list_survival_treatment_scores_kernel(
 
         place_scales(0, nc.scalar)
         w2q = [deal_w2(0, w2_first)]
-        w2_second = load_w2(1, "w2_raw")
         g_unit = held([P, UNIT, PACK], F32, "g_unit", "picked0")
         nc.vector.tensor_copy(g_unit[:], g_columns[:, :PACK].unsqueeze(1).to_broadcast([P, UNIT, PACK]))
-        w1_rest = held([P, PACK * PASS], F32, "w1_rest", "g_columns")
+        w1_rest = held([P, PACK * PASS], F32, "w1_rest", "w2_raw")
         cut = PACK * SECOND
         w1_second = [
             w1_rest[:, : PACK * cut].rearrange("p (j c) -> p j c", j=PACK),
             w1_rest[:, PACK * cut :].rearrange("p (j c) -> p j c", j=PACK),
         ]
         nc.sync.dma_start(w1_second[0], by_partition(w1[:, PASS : PASS + cut]))
+        w2_second = load_w2(1, "g_columns")
         nc.sync.dma_start(w1_second[1], by_partition(w1[:, PASS + cut :]))
         place_scales(1, nc.sync)
 
@@ -182,7 +182,7 @@ def tile_list_survival_treatment_scores_kernel(
         w3_raw = [load_rows(w3[0:PASS, :], "w3_raw0", "w1_lo"), load_rows(w3[PASS:, :], "w3_raw1", "w1_hi")]
         w1_second_bf = held([P, PACK * PASS], BF16, "w1_second_bf", "rounded_w")
         deal(on_scalar, w1_second_bf, w1_second[0], 0, 0, SECOND)
-        one = held([P, 1], F32, "one", "w2_raw")
+        one = held([P, 1], F32, "one", "g_columns")
         nc.gpsimd.memset(one[:], 1.0)
         deal(on_gpsimd, w1_second_bf, w1_second[1], SECOND, SECOND, P)
 
@@ -208,8 +208,7 @@ def tile_list_survival_treatment_scores_kernel(
 
         def follow_up(unit):
             s = unit // UNITS
-            b_banks = B_BANKS_EARLY if unit < UNITS // 2 else B_BANKS
-            pb = bank(b_banks[unit % len(b_banks)], [P, PACK, UNIT])
+            pb = bank(B_BANKS[unit % len(B_BANKS)], [P, PACK, UNIT])
             product(pb, lambda c0: w2q[s][:, 2 * c0 : 2 * (c0 + P)].bitcast(FP4X4), planes[:, s, :PASS], unit)
             return pb
 
@@ -316,7 +315,10 @@ def tile_list_survival_treatment_scores_kernel(
         rounded = held([P, S, PACK], BF16, "rounded")
 
         def round_y(copy, j0, j1):
-            copy(rounded[:, j0:j1, :], y_all[:, :, j0:j1].rearrange("p t n -> p n t"))
+            copy(
+                rounded[:, j0:j1, :].rearrange("p (c i) t -> p c t i", i=PACK),
+                y_all[:, :, j0:j1].rearrange("p t (c i) -> p c t i", i=PACK),
+            )
 
         def quantise_y(j0, j1):
             nc.vector.quantize_mx(
@@ -334,7 +336,5 @@ def tile_list_survival_treatment_scores_kernel(
         quantise_y(HALF + WIDE, S)
         for j0, j1 in CODE_STORES:
             nc.sync.dma_start(y_words[:, j0:j1], y_codes[:, j0:j1])
-        for q, queue in enumerate([nc.sync, nc.scalar, nc.sync, nc.scalar]):
-            queue.dma_start(
-                out_2[0, 4 * q : 4 * q + 4, :].bitcast(I32), y_scales[32 * q : 32 * q + 4, :].bitcast(I32)
-            )
+        for r, queue in enumerate([nc.scalar, nc.sync, nc.scalar, nc.sync]):
+            queue.dma_start(out_2[0, r:SCALE_ROWS:4, :].bitcast(I32), y_scales[r:P:32, :].bitcast(I32))

@@ -35,13 +35,14 @@ SPLITS = (32, 116)
 SECOND = 64
 W1_AFTER = 2
 W3_AFTER = UNITS
+H_AFTER = UNITS + 4
 B_AHEAD = 2
 CODE_STORES = [(0, 512), (512, 768), (768, 1024)]
 FINITE = 3.0e38
 
 A_BANKS, A_BANKS_LATE, A_LATE_FROM = (0, 1, 5, 6), (0, 1), UNITS + 4
 B_BANKS = (2, 3, 4)
-Y_BANKS = ((5, 6), (5, 6), (0, 1), (3,), (4,))
+Y_BANKS = ((5, 6), (3, 4), (0, 1), (2,), (5,))
 G_BANK, G_TURN_BANK = 7, 4
 
 
@@ -222,7 +223,7 @@ def tile_list_survival_treatment_scores_kernel(
                 pa = bank(a_banks[unit % len(a_banks)], [P, PACK, UNIT])
                 product(pa, lambda c0: w1q[s][0][:, c0 : c0 + P].bitcast(FP8X4), w1q[s][1], unit)
                 pb = b_ahead[unit] if unit < B_AHEAD else follow_up(unit)
-                if unit in (W1_AFTER, W3_AFTER):
+                if unit in (W1_AFTER, W3_AFTER, H_AFTER):
                     hazard = held([P, UNIT, PACK], F32, "hazard", f"after{unit}")
                 else:
                     hazard = ahead.tile([P, UNIT, PACK], F32, name="hazard")
@@ -235,7 +236,8 @@ def tile_list_survival_treatment_scores_kernel(
                     ALU.min,
                     ALU.mult,
                 )
-            xs[j0, s] = x
+            for u0 in range(0, width, UNIT):
+                xs[j0 + u0, s] = x[:, u0:width, :]
 
         def survive(j0, width, s):
             alive = work.tile([P, WIDE, PACK], F32, name="alive")
@@ -290,24 +292,26 @@ def tile_list_survival_treatment_scores_kernel(
                 w3_bf = held([P, PASSES * PACK * PASS], BF16, "w3_bf", "rounded_w")
                 for s in range(PASSES):
                     deal(on_gpsimd, w3_bf[:, s * PACK * PASS : (s + 1) * PACK * PASS], w3_raw[s][:], 0, 0, P)
-            survive(j0 - WIDE, WIDE, 0)
             if j0 - WIDE < ON_VECTOR * WIDE:
+                survive(j0 - WIDE, WIDE, 0)
                 weigh(j0 - WIDE, WIDE, 0)
 
         exposure(*GROUPS[0], 1)
         w3_codes, w3_scales = quantise("w3", w3_bf, PASSES * PASS, scales_tag=f"after{W3_AFTER}")
         w3q = [(w3_codes[:, s * PASS : (s + 1) * PASS], w3_scales[:, s * PASS : (s + 1) * PASS]) for s in range(PASSES)]
-        weigh_on_gpsimd(*GROUPS[ON_VECTOR], "rounded_w")
+        exposure(*GROUPS[1], 1)
+        last_read = "rounded_w"
         for c, (j0, width) in enumerate(GROUPS):
-            if c + 1 < len(GROUPS):
-                exposure(*GROUPS[c + 1], 1)
             survive(j0, width, 1)
+            if ON_VECTOR + c < len(GROUPS):
+                survive(*GROUPS[ON_VECTOR + c], 0)
+                weigh_on_gpsimd(*GROUPS[ON_VECTOR + c], last_read)
             weigh(j0, width, 1)
-            if c == 0:
-                survive(S - WIDE, WIDE, 0)
-            hq[j0] = quantise(f"h{j0}", h[j0][:].rearrange("p s n t -> p (s n t)"), PASSES * width)
-            if ON_VECTOR + 1 + c < len(GROUPS):
-                weigh_on_gpsimd(*GROUPS[ON_VECTOR + 1 + c], f"h{j0}")
+            if c + 2 < len(GROUPS):
+                exposure(*GROUPS[c + 2], 1)
+            values = h[j0][:].rearrange("p s n t -> p (s n t)")
+            hq[j0] = quantise(f"h{j0}", values, PASSES * width, scales_tag=None if c else f"after{H_AFTER}")
+            last_read = f"h{j0}"
 
         for (j0, width), y_banks in zip(GROUPS, Y_BANKS):
             scores(j0, width, y_banks)

@@ -280,7 +280,10 @@ def tile_list_survival_treatment_scores_kernel(
                         )
                 slots = slice(t0, t0 + per_bank)
                 nc.scalar.copy(y[:, slots, :], py[:])
-                nc.sync.dma_start(y_rows[:, slots, j0 : j0 + width], y[:, slots, :])
+                if width == WIDE:
+                    nc.sync.dma_start(y_rows[:, slots, j0 : j0 + width], y[:, slots, :])
+                elif j0 + width == S:
+                    nc.sync.dma_start(y_rows[:, :, S - WIDE :], y_all[:, :, S - WIDE :])
 
         exposure(0, WIDE, 0)
         g_bank = bank(G_BANK, [P, P])
@@ -340,5 +343,5 @@ def tile_list_survival_treatment_scores_kernel(
         quantise_y(HALF + WIDE, S)
         for j0, j1 in CODE_STORES:
             nc.sync.dma_start(y_words[:, j0:j1], y_codes[:, j0:j1])
-        for r, queue in enumerate([nc.scalar, nc.sync, nc.scalar, nc.sync]):
-            queue.dma_start(out_2[0, r:SCALE_ROWS:4, :].bitcast(I32), y_scales[r:P:32, :].bitcast(I32))
+        for r in range(4):
+            nc.scalar.dma_start(out_2[0, r:SCALE_ROWS:4, :].bitcast(I32), y_scales[r:P:32, :].bitcast(I32))

@@ -32,7 +32,7 @@ ON_VECTOR = 2
 ROUND_ON_SCALAR = 3
 PIECE = 96
 SPLITS = (32, 116)
-SECOND = 64
+SECOND = 48
 W1_AFTER = 2
 W3_AFTER = UNITS
 H_AFTER = UNITS + 4
@@ -164,21 +164,23 @@ def tile_list_survival_treatment_scores_kernel(
         nc.sync.dma_start(w1_second[1], by_partition(w1[:, PASS + cut :]))
         place_scales(1, nc.sync)
 
-        def pick_words(half, words):
-            cols = slice(half * HALF // 16, (half + 1) * HALF // 16)
+        def pick_words(first, words):
+            count = words.shape[1]
+            cols = slice(first // 16, (first + count) // 16)
             nc.vector.tensor_copy(words[:], tabw[:].bitcast(U32).indirect(offsets[:, cols]))
-            return words
+            return [words[:, lo : lo + UNIT] for lo in range(0, count, UNIT)]
 
-        vq = [pick_words(0, held([P, HALF], U32, "vq0"))]
+        vq = pick_words(0, held([P, HALF], U32, "vq0"))
         w1_first_bf = after_w1.tile([P, PACK * PASS], BF16, name="w1_first_bf", offset=0, align_bytes=64)
         deal(on_scalar, w1_first_bf, w1_lo[:], 0, 0, SPLITS[0])
         deal(on_vector, w1_first_bf, w1_lo[:], 0, SPLITS[0], PIECE)
         deal(on_vector, w1_first_bf, w1_hi[:], PIECE, PIECE, SPLITS[1])
         deal(on_scalar, w1_first_bf, w1_hi[:], PIECE, SPLITS[1], P)
         w1q = [quantise("w1_first", w1_first_bf, PASS, calls=2)]
+        vq.extend(pick_words(HALF, held([P, WIDE], U32, "vq1")))
         g_rows = after_w1.tile([P, P], F32, name="g_rows", offset=0, align_bytes=64)
         nc.vector.tensor_copy(g_rows[:], g_turned[:])
-        vq.append(pick_words(1, after_w1.tile([P, HALF], U32, name="vq1", offset=4 * HALF, align_bytes=64)))
+        vq.extend(pick_words(HALF + WIDE, after_w1.tile([P, WIDE], U32, name="vq2", offset=4 * HALF, align_bytes=64)))
         w2q.append(deal_w2(1, w2_second, "tabw"))
         w3_raw = [load_rows(w3[0:PASS, :], "w3_raw0", "w1_lo"), load_rows(w3[PASS:, :], "w3_raw1", "w1_hi")]
         w1_second_bf = held([P, PACK * PASS], BF16, "w1_second_bf", "rounded_w")
@@ -201,7 +203,7 @@ def tile_list_survival_treatment_scores_kernel(
                     out=out[:, t, :],
                     lhsT=codes(t * P),
                     lhsT_scale=scales[:, t * P : (t + 1) * P],
-                    rhs=vq[half][:, lo : lo + UNIT].bitcast(FP8X4),
+                    rhs=vq[unit % UNITS].bitcast(FP8X4),
                     rhs_scale=planes[:, half, PASS + lo : PASS + lo + UNIT],
                     start=True,
                     stop=True,

@@ -101,8 +101,8 @@ def tile_list_survival_treatment_scores_kernel(
             return raw
 
         def deal(copy, grouped, raw, first, lo, hi):
-            dst = grouped[:].rearrange("p (t m j) -> p m t j", t=PACK, j=PACK)
-            src = raw.rearrange("p j (m t) -> p m t j", t=PACK)
+            dst = grouped[:].rearrange("p (t m j) -> p m j t", t=PACK, j=PACK)
+            src = raw.rearrange("p j (m t) -> p m j t", t=PACK)
             copy(dst[:, lo:hi], src[:, lo - first : hi - first])
 
         def quantise(name, values, width, calls=1, codes_tag=None, scales_tag=None):

from contextlib import ExitStack

import concourse.mybir as mybir
from concourse.masks import make_identity

K, T, S, H, N = 512, 4096, 1024, 1024, 512
FLOPS = 2 * (2 * K * H * S + H * N * S)

F32 = mybir.dt.float32
BF16 = mybir.dt.bfloat16
I32 = mybir.dt.int32
U32 = mybir.dt.uint32
U16 = mybir.dt.uint16
U8 = mybir.dt.uint8
FP8X4 = mybir.dt.float8_e4m3fn_x4
FP4X4 = mybir.dt.float4_e2m1fn_x4
ALU = mybir.AluOpType
EXP = mybir.ActivationFunctionType.Exp

P = 128
PACK = 4
PASS = P * PACK
PASSES = H // PASS
SCALE_ROWS = PASS // 32
ROW0 = P - SCALE_ROWS
UNIT = PASS // PACK
UNITS = S // UNIT
HALF = S // 2
WIDE = 2 * UNIT
GROUPS = [(0, WIDE), (WIDE, WIDE), (2 * WIDE, WIDE), (3 * WIDE, UNIT), (3 * WIDE + UNIT, UNIT)]
ON_VECTOR = 2
ROUND_ON_SCALAR = 3
PIECE = 96
SPLITS = (32, 116)
SECOND = 48
W1_AFTER = 2
W3_AFTER = UNITS
H_AFTER = UNITS + 4
B_AHEAD = 2
CODE_STORES = [(0, 512), (512, 768), (768, 1024)]
FINITE = 3.0e38

A_BANKS, A_BANKS_LATE, A_LATE_FROM = (0, 1, 5, 6), (0, 1), UNITS + 4
B_BANKS = (2, 3, 4)
Y_BANKS = ((5, 6), (3, 4), (0, 1), (2,), (5,))
G_BANK, G_TURN_BANK = 7, 4


def tile_list_survival_treatment_scores_kernel(
    tc, tab_words, tab_scales, offs, w1, w2_words, w2_scales, g, w3, out_0, out_1, out_2
):
    nc = tc.nc
    with ExitStack() as ctx:
        lists = ctx.enter_context(tc.tile_pool(name="lists", bufs=1))
        keep = ctx.enter_context(tc.tile_pool(name="keep", bufs=1))
        work = ctx.enter_context(tc.tile_pool(name="work", bufs=4))
        ahead = ctx.enter_context(tc.tile_pool(name="ahead", bufs=6))
        after_w1 = ctx.enter_context(tc.tile_pool(name="after_w1", bufs=1))
        banks = ctx.enter_context(tc.psum_pool(name="banks", bufs=1))

        def bank(number, shape):
            return banks.tile(shape, F32, name=f"bank{number}", tag=f"bank{number}")

        def held(shape, dtype, name, tag=None):
            return keep.tile(shape, dtype, name=name, tag=tag or name, align_bytes=64)

        on_vector, on_scalar = nc.vector.tensor_copy, nc.scalar.copy

        def on_gpsimd(dst, src):
            nc.gpsimd.tensor_scalar(dst, src, one[:], 0.0, ALU.mult, ALU.add)

        offsets = lists.tile([P, S // 16], U16, name="offsets")
        nc.sync.dma_start(offsets[:], offs)

        tabs = held([P, T], U8, "tabs")
        nc.sync.dma_start(tabs[ROW0:, :].bitcast(I32), tab_scales[0].bitcast(I32))
        nc.vector.memset(tabs[:ROW0, :].bitcast(I32), 0)
        w2s_raw = held([P, H], U8, "w2s_raw")
        nc.sync.dma_start(w2s_raw[ROW0:, :].bitcast(I32), w2_scales[0].bitcast(I32))
        nc.vector.memset(w2s_raw[:ROW0, :].bitcast(I32), 0)
        planes = held([P, 2, PASS + HALF], U8, "planes")
        nc.vector.memset(planes[:].rearrange("p i c -> p (i c)").bitcast(I32), 0)

        g_columns = held([P, P], F32, "g_columns")
        nc.scalar.dma_start(
            g_columns[:, : PASSES * PACK].rearrange("p (s t) -> p s t", t=PACK),
            g.rearrange("(s p t) -> p s t", t=PACK, p=P),
        )
        nc.vector.memset(g_columns[:, PASSES * PACK :], 0.0)
        identity = keep.tile([P, P], F32, name="identity")
        make_identity(nc, identity[:])
        g_turned = bank(G_TURN_BANK, [P, P])
        nc.tensor.transpose(g_turned[:], g_columns[:], identity[:])

        def by_partition(rows):
            return rows.rearrange("(p j) c -> p j c", j=PACK)

        def load_rows(rows, name, tag):
            raw = held([P, PACK, rows.shape[1]], F32, name, tag)
            nc.sync.dma_start(raw[:], by_partition(rows))
            return raw

        def deal(copy, grouped, raw, first, lo, hi):
            dst = grouped[:].rearrange("p (t m j) -> p m j t", t=PACK, j=PACK)
            src = raw.rearrange("p j (m t) -> p m j t", t=PACK)
            copy(dst[:, lo:hi], src[:, lo - first : hi - first])

        def quantise(name, values, width, calls=1, codes_tag=None, scales_tag=None):
            codes = held([P, width], U32, name + "_codes", codes_tag)
            scales = held([P, width], U8, name + "_scales", scales_tag)
            step = width // calls
            for c0 in range(0, width, step):
                nc.vector.quantize_mx(
                    out=codes[:, c0 : c0 + step].bitcast(FP8X4),
                    scales=scales[:, c0 : c0 + step],
                    in_=values[:, PACK * c0 : PACK * (c0 + step)],
                )
            return codes, scales

        def place_scales(part, queue):
            picked = held([P, HALF], U8, f"picked{part}")
            cols = slice(part * HALF // 16, (part + 1) * HALF // 16)
            nc.vector.tensor_copy(picked[:], tabs[:].indirect(offsets[:, cols]))
            staged = held([P, PASS + HALF], U8, f"staged{part}")
            nc.vector.tensor_copy(
                staged[:, :PASS].rearrange("p (t m) -> p t m", t=PACK),
                w2s_raw[:, part * PASS : (part + 1) * PASS].rearrange("p (m t) -> p t m", t=PACK),
            )
            nc.vector.tensor_copy(staged[:, PASS:].bitcast(I32), picked[:].bitcast(I32))
            for r in range(4):
                queue.dma_start(planes[r:P:32, part, :].bitcast(I32), staged[ROW0 + r : P : 4, :].bitcast(I32))

        def load_w2(s, tag):
            raw = held([P, 2 * PASS], U8, f"w2_raw{s}", tag)
            nc.sync.dma_start(raw[:].bitcast(I32), w2_words[0, :, 2 * s * PASS : 2 * (s + 1) * PASS].bitcast(I32))
            return raw

        def deal_w2(s, raw, tag=None):
            words = held([P, 2 * PASS], U8, f"w2q{s}", tag)
            nc.vector.tensor_copy(
                words[:].bitcast(U16).rearrange("p (t m) -> p t m", t=PACK),
                raw[:].bitcast(U16).rearrange("p (m t) -> p t m", t=PACK),
            )
            return words

        w2_first = load_w2(0, "w2_raw")
        tabw = held([P, T], I32, "tabw")
        nc.sync.dma_start(tabw[:], tab_words[0].rearrange("p t i -> p (t i)").bitcast(I32))
        w1_lo = load_rows(w1[:, 0 : PACK * PIECE], "w1_lo", "w1_lo")
        w1_hi = load_rows(w1[:, PACK * PIECE : PASS], "w1_hi", "w1_hi")

        place_scales(0, nc.scalar)
        w2q = [deal_w2(0, w2_first)]
        g_unit = held([P, UNIT, PACK], F32, "g_unit", "picked0")
        nc.vector.tensor_copy(g_unit[:], g_columns[:, :PACK].unsqueeze(1).to_broadcast([P, UNIT, PACK]))
        w1_rest = held([P, PACK * PASS], F32, "w1_rest", "w2_raw")
        cut = PACK * SECOND
        w1_second = [
            w1_rest[:, : PACK * cut].rearrange("p (j c) -> p j c", j=PACK),
            w1_rest[:, PACK * cut :].rearrange("p (j c) -> p j c", j=PACK),
        ]
        nc.sync.dma_start(w1_second[0], by_partition(w1[:, PASS : PASS + cut]))
        w2_second = load_w2(1, "g_columns")
        nc.sync.dma_start(w1_second[1], by_partition(w1[:, PASS + cut :]))
        place_scales(1, nc.sync)

        def pick_words(first, words):
            count = words.shape[1]
            cols = slice(first // 16, (first + count) // 16)
            nc.vector.tensor_copy(words[:], tabw[:].bitcast(U32).indirect(offsets[:, cols]))
            return [words[:, lo : lo + UNIT] for lo in range(0, count, UNIT)]

        vq = pick_words(0, held([P, HALF], U32, "vq0"))
        w1_first_bf = after_w1.tile([P, PACK * PASS], BF16, name="w1_first_bf", offset=0, align_bytes=64)
        deal(on_scalar, w1_first_bf, w1_lo[:], 0, 0, SPLITS[0])
        deal(on_vector, w1_first_bf, w1_lo[:], 0, SPLITS[0], PIECE)
        deal(on_vector, w1_first_bf, w1_hi[:], PIECE, PIECE, SPLITS[1])
        deal(on_scalar, w1_first_bf, w1_hi[:], PIECE, SPLITS[1], P)
        w1q = [quantise("w1_first", w1_first_bf, PASS, calls=2)]
        vq.extend(pick_words(HALF, held([P, WIDE], U32, "vq1")))
        g_rows = after_w1.tile([P, P], F32, name="g_rows", offset=0, align_bytes=64)
        nc.vector.tensor_copy(g_rows[:], g_turned[:])
        vq.extend(pick_words(HALF + WIDE, after_w1.tile([P, WIDE], U32, name="vq2", offset=4 * HALF, align_bytes=64)))
        w2q.append(deal_w2(1, w2_second, "tabw"))
        w3_raw = [load_rows(w3[0:PASS, :], "w3_raw0", "w1_lo"), load_rows(w3[PASS:, :], "w3_raw1", "w1_hi")]
        w1_second_bf = held([P, PACK * PASS], BF16, "w1_second_bf", "rounded_w")
        deal(on_scalar, w1_second_bf, w1_second[0], 0, 0, SECOND)
        one = held([P, 1], F32, "one", "g_columns")
        nc.gpsimd.memset(one[:], 1.0)
        deal(on_gpsimd, w1_second_bf, w1_second[1], SECOND, SECOND, P)

        y_all = keep.tile([P, PACK, S], F32, name="y_all")
        y_scales = held([P, S], U8, "y_scales")
        y_codes = held([P, S], I32, "y_codes")
        y_rows = out_0.rearrange("(p t) j -> p t j", t=PACK)
        y_words = out_1[0].rearrange("p m t -> p (m t)").bitcast(I32)
        xs, alives, h, hq = {}, {}, {}, {}

        def product(out, codes, scales, unit):
            half, lo = divmod(unit % UNITS * UNIT, HALF)
            for t in range(PACK):
                nc.tensor.matmul_mx(
                    out=out[:, t, :],
                    lhsT=codes(t * P),
                    lhsT_scale=scales[:, t * P : (t + 1) * P],
                    rhs=vq[unit % UNITS].bitcast(FP8X4),
                    rhs_scale=planes[:, half, PASS + lo : PASS + lo + UNIT],
                    start=True,
                    stop=True,
                )

        def follow_up(unit):
            s = unit // UNITS
            pb = bank(B_BANKS[unit % len(B_BANKS)], [P, PACK, UNIT])
            product(pb, lambda c0: w2q[s][:, 2 * c0 : 2 * (c0 + P)].bitcast(FP4X4), planes[:, s, :PASS], unit)
            return pb

        b_ahead = [follow_up(unit) for unit in range(B_AHEAD)]

        def exposure(j0, width, s):
            x = ahead.tile([P, WIDE, PACK], F32, name="x")
            for u0 in range(0, width, UNIT):
                unit = s * UNITS + (j0 + u0) // UNIT
                a_banks = A_BANKS if unit < A_LATE_FROM else A_BANKS_LATE
                pa = bank(a_banks[unit % len(a_banks)], [P, PACK, UNIT])
                product(pa, lambda c0: w1q[s][0][:, c0 : c0 + P].bitcast(FP8X4), w1q[s][1], unit)
                pb = b_ahead[unit] if unit < B_AHEAD else follow_up(unit)
                if unit in (W1_AFTER, W3_AFTER, H_AFTER):
                    hazard = held([P, UNIT, PACK], F32, "hazard", f"after{unit}")
                else:
                    hazard = ahead.tile([P, UNIT, PACK], F32, name="hazard")
                nc.scalar.activation(hazard[:], pa[:].rearrange("p t n -> p n t"), EXP)
                nc.vector.scalar_tensor_tensor(
                    x[:, u0 : u0 + UNIT, :],
                    hazard[:],
                    FINITE,
                    pb[:].rearrange("p t n -> p n t"),
                    ALU.min,
                    ALU.mult,
                )
            for u0 in range(0, width, UNIT):
                xs[j0 + u0, s] = x[:, u0:width, :]

        def survive(j0, width, s):
            alive = work.tile([P, WIDE, PACK], F32, name="alive")
            nc.scalar.activation(alive[:, :width, :], xs[j0, s][:, :width, :], EXP, scale=-1.0)
            for u0 in range(0, width, UNIT):
                alives[j0 + u0, s] = alive[:, u0:width, :]

        def weigh(j0, width, s):
            if s == 0:
                h[j0] = held([P, PASSES, width, PACK], BF16, f"h{j0}")
            factors = g_bank[:, s * PACK : (s + 1) * PACK].unsqueeze(1).to_broadcast([P, width, PACK])
            nc.vector.tensor_tensor(h[j0][:, s], alives[j0, s][:, :width, :], factors, ALU.mult)

        def weigh_on_gpsimd(j0, width, tag):
            h[j0] = held([P, PASSES, width, PACK], BF16, f"h{j0}", tag)
            units = width // UNIT
            nc.gpsimd.tensor_tensor(
                h[j0][:, 0].rearrange("p (u n) t -> p u (n t)", u=units),
                alives[j0, 0][:, :width, :].rearrange("p (u n) t -> p u (n t)", u=units),
                g_unit[:].rearrange("p n t -> p (n t)").unsqueeze(1).to_broadcast([P, units, UNIT * PACK]),
                ALU.mult,
            )

        def scores(j0, width, y_banks):
            per_bank = PASS // width
            y = y_all[:, :, j0 : j0 + width]
            for t0 in range(0, PACK, per_bank):
                py = bank(y_banks[t0 // per_bank], [P, per_bank, width])
                for t in range(t0, t0 + per_bank):
                    cols = slice(t * P, (t + 1) * P)
                    for s in range(PASSES):
                        nc.tensor.matmul_mx(
                            out=py[:, t - t0, :],
                            lhsT=w3q[s][0][:, cols].bitcast(FP8X4),
                            lhsT_scale=w3q[s][1][:, cols],
                            rhs=hq[j0][0][:, s * width : (s + 1) * width].bitcast(FP8X4),
                            rhs_scale=hq[j0][1][:, s * width : (s + 1) * width],
                            start=(s == 0),
                            stop=(s == PASSES - 1),
                        )
                slots = slice(t0, t0 + per_bank)
                nc.scalar.copy(y[:, slots, :], py[:])
                if width == WIDE:
                    nc.sync.dma_start(y_rows[:, slots, j0 : j0 + width], y[:, slots, :])
                elif j0 + width == S:
                    nc.sync.dma_start(y_rows[:, :, S - WIDE :], y_all[:, :, S - WIDE :])

        exposure(0, WIDE, 0)
        g_bank = bank(G_BANK, [P, P])
        nc.tensor.transpose(g_bank[:], g_rows[:], identity[:])
        for j0 in range(WIDE, S, WIDE):
            exposure(j0, WIDE, 0)
            if j0 == WIDE:
                w1q.append(quantise("w1_second", w1_second_bf, PASS, scales_tag=f"after{W1_AFTER}"))
                w3_bf = held([P, PASSES * PACK * PASS], BF16, "w3_bf", "rounded_w")
                for s in range(PASSES):
                    deal(on_gpsimd, w3_bf[:, s * PACK * PASS : (s + 1) * PACK * PASS], w3_raw[s][:], 0, 0, P)
            if j0 - WIDE < ON_VECTOR * WIDE:
                survive(j0 - WIDE, WIDE, 0)
                weigh(j0 - WIDE, WIDE, 0)

        exposure(*GROUPS[0], 1)
        w3_codes, w3_scales = quantise("w3", w3_bf, PASSES * PASS, scales_tag=f"after{W3_AFTER}")
        w3q = [(w3_codes[:, s * PASS : (s + 1) * PASS], w3_scales[:, s * PASS : (s + 1) * PASS]) for s in range(PASSES)]
        exposure(*GROUPS[1], 1)
        last_read = "rounded_w"
        for c, (j0, width) in enumerate(GROUPS):
            survive(j0, width, 1)
            if ON_VECTOR + c < len(GROUPS):
                survive(*GROUPS[ON_VECTOR + c], 0)
                weigh_on_gpsimd(*GROUPS[ON_VECTOR + c], last_read)
            weigh(j0, width, 1)
            if c + 2 < len(GROUPS):
                exposure(*GROUPS[c + 2], 1)
            values = h[j0][:].rearrange("p s n t -> p (s n t)")
            hq[j0] = quantise(f"h{j0}", values, PASSES * width, scales_tag=None if c else f"after{H_AFTER}")
            last_read = f"h{j0}"

        for (j0, width), y_banks in zip(GROUPS, Y_BANKS):
            scores(j0, width, y_banks)

        rounded = held([P, S, PACK], BF16, "rounded")

        def round_y(copy, j0, j1):
            copy(
                rounded[:, j0:j1, :].rearrange("p (c i) t -> p c t i", i=PACK),
                y_all[:, :, j0:j1].rearrange("p t (c i) -> p c t i", i=PACK),
            )

        def quantise_y(j0, j1):
            nc.vector.quantize_mx(
                out=y_codes[:, j0:j1].bitcast(FP8X4),
                scales=y_scales[:, j0:j1],
                in_=rounded[:, j0:j1, :].rearrange("p n t -> p (n t)"),
            )

        round_y(on_vector, 0, HALF)
        round_y(on_vector, HALF, HALF + WIDE)
        quantise_y(0, HALF)
        round_y(on_scalar, HALF + WIDE, S - UNIT)
        round_y(on_vector, S - UNIT, S)
        quantise_y(HALF, HALF + WIDE)
        quantise_y(HALF + WIDE, S)
        for j0, j1 in CODE_STORES:
            nc.sync.dma_start(y_words[:, j0:j1], y_codes[:, j0:j1])
        for r in range(4):
            nc.scalar.dma_start(out_2[0, r:SCALE_ROWS:4, :].bitcast(I32), y_scales[r:P:32, :].bitcast(I32))
